import numpy as np
import ml_dtypes


def mxq(x, axis, fmt="e4m3"):
    dtype, down = {"e4m3": (ml_dtypes.float8_e4m3fn, 7), "e5m2": (ml_dtypes.float8_e5m2, 14)}[fmt]
    v = np.moveaxis(np.asarray(x, np.float32).astype(ml_dtypes.bfloat16).astype(np.float64), axis, -1)
    blocks = v.reshape(v.shape[:-1] + (-1, 32))
    amax = np.abs(blocks).max(-1, keepdims=True)
    byte = np.maximum(np.where(amax > 0, np.frexp(amax)[1] - 1 + 127, 0) - down, 1)
    scale = np.exp2(byte - 127.0)
    codes = (blocks / scale).astype(np.float32).astype(dtype).astype(np.float64)
    return np.moveaxis((codes * scale).reshape(v.shape), -1, axis)


WIDE = False


def mx_kscale(k):
    if not WIDE:
        return np.ones(k)
    levels = np.array([10, -10, 5, -5, 0])
    if k % 512:
        return np.exp2(np.random.permutation(np.resize(levels, k // 32))).repeat(32)
    a = np.empty((k // 512, 16))
    for p in range(k // 512):
        a[p, :8] = np.random.permutation(np.resize(levels, 8))
        for g in range(8):
            far = levels[np.abs(levels - a[p, g]) >= 10]
            a[p, g + 8] = far[np.random.randint(len(far))]
    return np.exp2(a.ravel()).repeat(32)


def f64(x):
    return np.asarray(x).astype(np.float64)


def striped(idx):
    return np.tile(idx.reshape(-1, 16).T, (8, 1)).astype(np.uint16)


def unstriped(offs):
    return offs[:16].T.reshape(-1).astype(np.int64)


E2M1 = np.array([0.0, 0.5, 1.0, 1.5, 2.0, 3.0, 4.0, 6.0, -0.0, -0.5, -1.0, -1.5, -2.0, -3.0, -4.0, -6.0])


def pack_fp4(w):
    k, n = w.shape
    w = f64(np.asarray(w, np.float32).astype(ml_dtypes.bfloat16)).reshape(k // 32, 32, n)
    amax = np.abs(w).max(1)
    mant, ex = np.frexp(amax / 6.0)
    byte = np.clip(np.where(amax > 0, np.where(mant > 0.5, ex, ex - 1) + 127, 1), 1, 254)
    scaled = (w * np.exp2(127.0 - byte)[:, None, :]).reshape(k, n).astype(np.float32)
    c = np.ascontiguousarray(scaled.reshape(k // 512, 128, 4, n).transpose(0, 1, 3, 2)).astype(ml_dtypes.float4_e2m1fn).view(np.uint8) & 0xF
    words = (c[..., 0::2] | (c[..., 1::2] << 4)).reshape(k // 512, 128, 2 * n)
    return np.ascontiguousarray(words), np.ascontiguousarray(byte.astype(np.uint8).reshape(k // 512, 16, n))


def unpack_fp4(words, scales):
    g, _, n = scales.shape
    words = np.ascontiguousarray(words).reshape(g, 128, n, 2)
    nib = np.empty((g, 128, n, 4), np.uint8)
    nib[..., 0::2] = words & 0xF
    nib[..., 1::2] = words >> 4
    vals = E2M1[nib] * np.repeat(np.exp2(scales.astype(np.float64) - 127.0), 8, axis=1)[..., None]
    return vals.transpose(0, 1, 3, 2).reshape(g * 512, n)


def relu(v):
    return np.maximum(v, 0.0)


K, T, S, V, N = 512, 1024, 512, 256, 256


def setup_inputs():
    n = np.random.standard_normal
    s = mx_kscale(K)[:, None]
    packed_w1 = pack_fp4(n((K, N)) / np.sqrt(K) / s)
    packed_w2 = pack_fp4(n((K, N)) / np.sqrt(K) / s)
    packed_w3 = pack_fp4(n((K, N)) / np.sqrt(K) / s)
    return {
        "xT": (n((K, T)) * s).astype(np.float32),
        "w1_words": packed_w1[0],
        "w1_scales": packed_w1[1],
        "w2_words": packed_w2[0],
        "w2_scales": packed_w2[1],
        "w3_words": packed_w3[0],
        "w3_scales": packed_w3[1],
        "offs": striped(np.random.permutation(T)[:S]),
        "cen": striped(np.random.permutation(S)[:V]),
        "pos1": striped(np.random.permutation(S)[:V]),
        "pos2": striped(np.random.permutation(S)[:V]),
        "pos3": striped(np.random.permutation(S)[:V]),
    }


def reference(xT, w1_words, w1_scales, w2_words, w2_scales, w3_words, w3_scales, offs, cen, pos1, pos2, pos3):
    xq = mxq(f64(xT)[:, unstriped(offs)], 0, "e4m3")
    h = unpack_fp4(w3_words, w3_scales).T @ xq
    g = unpack_fp4(w1_words, w1_scales).T @ xq
    gc = g[:, unstriped(cen)]
    s = unpack_fp4(w2_words, w2_scales).T @ xq
    sc = s[:, unstriped(cen)]
    return relu(h[:, unstriped(pos1)] * gc + sc) + relu(h[:, unstriped(pos2)] * gc + sc) + relu(h[:, unstriped(pos3)] * gc + sc)

@@ -1,0 +1,148 @@
+from contextlib import ExitStack
+
+import concourse.mybir as mybir
+
+K, T, S, V, N = 512, 1024, 512, 256, 256
+FLOPS = 3 * 2 * K * S * N
+
+F32 = mybir.dt.float32
+BF16 = mybir.dt.bfloat16
+I32 = mybir.dt.int32
+U32 = mybir.dt.uint32
+U16 = mybir.dt.uint16
+U8 = mybir.dt.uint8
+FP8X4 = mybir.dt.float8_e4m3fn_x4
+FP4X4 = mybir.dt.float4_e2m1fn_x4
+ALU = mybir.AluOpType
+ACT = mybir.ActivationFunctionType
+
+P = 128
+HALF = S // 2
+
+
+def tile_picked_filmg_relu_e_kernel(
+    tc, xT, w1_words, w1_scales, w2_words, w2_scales, w3_words, w3_scales, offs, cen, pos1, pos2, pos3, out
+):
+    nc = tc.nc
+    with ExitStack() as ctx:
+        keep = ctx.enter_context(tc.tile_pool(name="keep", bufs=1))
+        psum = ctx.enter_context(tc.psum_pool(name="psum", bufs=8))
+
+        def load_list(name, src):
+            tile = keep.tile(list(src.shape), U16, name=name)
+            nc.sync.dma_start(tile[:], src)
+            return tile
+
+        scales = {}
+        for name in "ghs":
+            scales[name] = keep.tile([P, N], U8, name="scales_" + name, align_bytes=64)
+            nc.gpsimd.memset(scales[name][:].bitcast(I32), 0)
+
+        offs_sb = load_list("offs_sb", offs)
+
+        x_rows = xT.rearrange("(p j) t -> p j t", j=4)
+        chunks = [(0, 0, 512), (0, 512, 1024), (1, 0, 512), (1, 512, 768), (1, 768, 1024)]
+        raw = []
+        for u, c0, c1 in chunks:
+            tile = keep.tile([P, 2, c1 - c0], F32, name="raw%d_%d" % (u, c0))
+            nc.sync.dma_start(tile[:], x_rows[:, 2 * u : 2 * u + 2, c0:c1])
+            raw.append(tile)
+
+        words = {}
+
+        def load_weights(name, w_words, w_scales, queue):
+            words[name] = keep.tile([P, 2 * N], U8, name="words_" + name, align_bytes=64)
+            nc.sync.dma_start(words[name][:].bitcast(I32), w_words[0].bitcast(I32))
+            for q in range(4):
+                queue.dma_start(
+                    scales[name][32 * q : 32 * q + 4, :].bitcast(I32), w_scales[0, 4 * q : 4 * q + 4, :].bitcast(I32)
+                )
+
+        load_weights("g", w1_words, w1_scales, nc.gpsimd)
+        load_weights("h", w3_words, w3_scales, nc.sync)
+        load_weights("s", w2_words, w2_scales, nc.sync)
+        cen_sb = load_list("cen_sb", cen)
+        pos_sb = [load_list("pos%d_sb" % d, src) for d, src in enumerate((pos1, pos2, pos3))]
+
+        pairs = [keep.tile([P, 2 * T], BF16, name="pairs%d" % u, align_bytes=64) for u in range(2)]
+
+        def cast(i, on_scalar):
+            u, c0, c1 = chunks[i]
+            dst = pairs[u][:, 2 * c0 : 2 * c1].rearrange("p (t e) -> p t e", e=2)
+            src = raw[i][:].rearrange("p e t -> p t e")
+            if on_scalar:
+                nc.scalar.activation(dst, src, ACT.Copy)
+            else:
+                nc.vector.tensor_copy(dst, src)
+
+        picked = [keep.tile([P, 2 * HALF], U32, name="picked%d" % a) for a in range(2)]
+
+        def gather_pairs(u, a):
+            nc.vector.tensor_copy(
+                picked[a][:, u * HALF : (u + 1) * HALF],
+                pairs[u][:].bitcast(U32).indirect(offs_sb[:, 16 * a : 16 * (a + 1)]),
+            )
+
+        cast(0, True)
+        cast(1, False)
+        gather_pairs(0, 0)
+        gather_pairs(0, 1)
+        cast(2, True)
+        cast(3, False)
+        cast(4, False)
+        gather_pairs(1, 0)
+        gather_pairs(1, 1)
+
+        woven = [keep.tile([P, 4 * HALF], BF16, name="woven%d" % a, align_bytes=64) for a in range(2)]
+        nc.scalar.copy(
+            woven[0][:].bitcast(U32).rearrange("p (t u) -> p t u", u=2),
+            picked[0][:].rearrange("p (u t) -> p t u", u=2),
+        )
+        nc.vector.tensor_copy(
+            woven[1][:].bitcast(I32).rearrange("p (t u) -> p t u", u=2),
+            picked[1][:].bitcast(I32).rearrange("p (u t) -> p t u", u=2),
+        )
+        codes = [keep.tile([P, HALF], U32, name="codes%d" % a, align_bytes=64) for a in range(2)]
+        xscale = [keep.tile([P, HALF], U8, name="xscale%d" % a, align_bytes=64) for a in range(2)]
+        for a in range(2):
+            nc.vector.quantize_mx(out=codes[a][:].bitcast(FP8X4), scales=xscale[a][:], in_=woven[a][:])
+
+        rows = {}
+
+        def product(name, b):
+            rows[name, b] = keep.tile([P, S], F32, name="rows_%s%d" % (name, b))
+            for a in range(2):
+                bank = psum.tile([P, HALF], F32, name="bank")
+                nc.tensor.matmul_mx(
+                    out=bank[:],
+                    lhsT=words[name][:, 2 * P * b : 2 * P * (b + 1)].bitcast(FP4X4),
+                    lhsT_scale=scales[name][:, P * b : P * (b + 1)],
+                    rhs=codes[a][:].bitcast(FP8X4),
+                    rhs_scale=xscale[a][:],
+                    start=True,
+                    stop=True,
+                )
+                nc.scalar.activation(rows[name, b][:, a * HALF : (a + 1) * HALF], bank[:], ACT.Copy)
+
+        for b in range(2):
+            for name in "ghs":
+                product(name, b)
+
+        for b in range(2):
+            gc = keep.tile([P, V], F32, name="gc%d" % b)
+            sc = keep.tile([P, V], F32, name="sc%d" % b)
+            nc.vector.tensor_copy(gc[:], rows["g", b][:].indirect(cen_sb[:]))
+            t = [keep.tile([P, V], F32, name="t%d_%d" % (b, d)) for d in range(3)]
+            u = [keep.tile([P, V], F32, name="u%d_%d" % (b, d)) for d in range(3)]
+            r = [keep.tile([P, V], F32, name="r%d_%d" % (b, d)) for d in range(3)]
+            nc.vector.tensor_tensor(t[0][:], rows["h", b][:].indirect(pos_sb[0][:]), gc[:], ALU.mult)
+            nc.vector.tensor_copy(sc[:], rows["s", b][:].indirect(cen_sb[:]))
+            nc.vector.tensor_tensor(t[1][:], rows["h", b][:].indirect(pos_sb[1][:]), gc[:], ALU.mult)
+            nc.vector.tensor_tensor(u[0][:], t[0][:], sc[:], ALU.add)
+            nc.scalar.activation(r[0][:], u[0][:], ACT.Relu)
+            nc.vector.tensor_tensor(t[2][:], rows["h", b][:].indirect(pos_sb[2][:]), gc[:], ALU.mult)
+            nc.vector.tensor_tensor(u[1][:], t[1][:], sc[:], ALU.add)
+            nc.vector.tensor_tensor(u[2][:], t[2][:], sc[:], ALU.add)
+            nc.vector.scalar_tensor_tensor(r[1][:], u[1][:], 0.0, r[0][:], ALU.max, ALU.add)
+            nc.vector.scalar_tensor_tensor(r[2][:], u[2][:], 0.0, r[1][:], ALU.max, ALU.add)
+            nc.sync.dma_start(out[P * b : P * (b + 1), :], r[2][:])

@@ -1,6 +1,7 @@
 from contextlib import ExitStack
 
 import concourse.mybir as mybir
+from concourse.masks import make_identity
 
 K, T, S, V, N = 512, 1024, 512, 256, 256
 FLOPS = 3 * 2 * K * S * N
@@ -17,7 +18,6 @@ ALU = mybir.AluOpType
 ACT = mybir.ActivationFunctionType
 
 P = 128
-HALF = S // 2
 
 
 def tile_picked_filmg_relu_e_kernel(
@@ -26,123 +26,152 @@ def tile_picked_filmg_relu_e_kernel(
     nc = tc.nc
     with ExitStack() as ctx:
         keep = ctx.enter_context(tc.tile_pool(name="keep", bufs=1))
-        psum = ctx.enter_context(tc.psum_pool(name="psum", bufs=8))
+        psum = ctx.enter_context(tc.psum_pool(name="psum", bufs=1))
 
         def load_list(name, src):
             tile = keep.tile(list(src.shape), U16, name=name)
             nc.sync.dma_start(tile[:], src)
             return tile
 
-        scales = {}
-        for name in "ghs":
-            scales[name] = keep.tile([P, N], U8, name="scales_" + name, align_bytes=64)
-            nc.gpsimd.memset(scales[name][:].bitcast(I32), 0)
+        weights = {"g": (w1_words, w1_scales), "s": (w2_words, w2_scales), "h": (w3_words, w3_scales)}
+        scales = {name: keep.tile([P, N], U8, name="scales_" + name, align_bytes=64) for name in "gsh"}
+        words = {name: keep.tile([P, 2 * N], U8, name="words_" + name, align_bytes=64) for name in "gsh"}
 
-        offs_sb = load_list("offs_sb", offs)
+        def load_words(name):
+            nc.sync.dma_start(words[name][:].bitcast(I32), weights[name][0][0].bitcast(I32))
 
-        x_rows = xT.rearrange("(p j) t -> p j t", j=4)
-        chunks = [(0, 0, 512), (0, 512, 1024), (1, 0, 512), (1, 512, 768), (1, 768, 1024)]
-        raw = []
-        for u, c0, c1 in chunks:
-            tile = keep.tile([P, 2, c1 - c0], F32, name="raw%d_%d" % (u, c0))
-            nc.sync.dma_start(tile[:], x_rows[:, 2 * u : 2 * u + 2, c0:c1])
-            raw.append(tile)
-
-        words = {}
-
-        def load_weights(name, w_words, w_scales, queue):
-            words[name] = keep.tile([P, 2 * N], U8, name="words_" + name, align_bytes=64)
-            nc.sync.dma_start(words[name][:].bitcast(I32), w_words[0].bitcast(I32))
+        def load_scales(name, queue):
             for q in range(4):
                 queue.dma_start(
-                    scales[name][32 * q : 32 * q + 4, :].bitcast(I32), w_scales[0, 4 * q : 4 * q + 4, :].bitcast(I32)
+                    scales[name][32 * q : 32 * q + 32, :].bitcast(I32),
+                    weights[name][1][0, 4 * q : 4 * q + 4, :].bitcast(I32).unsqueeze(0).to_broadcast([8, 4, N // 4]),
                 )
 
-        load_weights("g", w1_words, w1_scales, nc.gpsimd)
-        load_weights("h", w3_words, w3_scales, nc.sync)
-        load_weights("s", w2_words, w2_scales, nc.sync)
+        offs_sb = load_list("offs_sb", offs)
+        x_rows = xT.rearrange("(p j) t -> p j t", j=4)
+        planes = []
+        for j in range(4):
+            plane = keep.tile([P, T], F32, name="plane%d" % j)
+            nc.sync.dma_start(plane[:], x_rows[:, j, :])
+            planes.append(plane)
+
+        load_words("g")
+        load_scales("g", nc.sync)
+        load_words("s")
+        load_scales("s", nc.sync)
+        load_words("h")
+        load_scales("h", nc.sync)
         cen_sb = load_list("cen_sb", cen)
         pos_sb = [load_list("pos%d_sb" % d, src) for d, src in enumerate((pos1, pos2, pos3))]
 
-        pairs = [keep.tile([P, 2 * T], BF16, name="pairs%d" % u, align_bytes=64) for u in range(2)]
+        ident = keep.tile([P, P], F32)
+        make_identity(nc, ident[:])
 
-        def cast(i, on_scalar):
-            u, c0, c1 = chunks[i]
-            dst = pairs[u][:, 2 * c0 : 2 * c1].rearrange("p (t e) -> p t e", e=2)
-            src = raw[i][:].rearrange("p e t -> p t e")
-            if on_scalar:
-                nc.scalar.activation(dst, src, ACT.Copy)
+        pieces = [(0, 256), (256, 512)]
+        picked = [keep.tile([P, 2 * S], BF16, name="picked%d" % u) for u in range(2)]
+        woven = [keep.tile([P, 4 * (b - a)], BF16, name="woven%d" % a, align_bytes=64) for a, b in pieces]
+
+        def gather(j, a, b):
+            u, e = divmod(j, 2)
+            nc.vector.tensor_copy(picked[u][:, e * S + a : e * S + b], planes[j][:].indirect(offs_sb[:, a // 16 : b // 16]))
+
+        def weave(u, i):
+            a, b = pieces[i]
+            dst = woven[i][:].rearrange("p (t j) -> p t j", j=4)[:, :, 2 * u : 2 * u + 2]
+            src = picked[u][:].rearrange("p (e t) -> p t e", e=2)[:, a:b, :]
+            if u == 0:
+                nc.scalar.copy(dst, src)
             else:
                 nc.vector.tensor_copy(dst, src)
 
-        picked = [keep.tile([P, 2 * HALF], U32, name="picked%d" % a) for a in range(2)]
-
-        def gather_pairs(u, a):
-            nc.vector.tensor_copy(
-                picked[a][:, u * HALF : (u + 1) * HALF],
-                pairs[u][:].bitcast(U32).indirect(offs_sb[:, 16 * a : 16 * (a + 1)]),
-            )
-
-        cast(0, True)
-        cast(1, False)
-        gather_pairs(0, 0)
-        gather_pairs(0, 1)
-        cast(2, True)
-        cast(3, False)
-        cast(4, False)
-        gather_pairs(1, 0)
-        gather_pairs(1, 1)
-
-        woven = [keep.tile([P, 4 * HALF], BF16, name="woven%d" % a, align_bytes=64) for a in range(2)]
-        nc.scalar.copy(
-            woven[0][:].bitcast(U32).rearrange("p (t u) -> p t u", u=2),
-            picked[0][:].rearrange("p (u t) -> p t u", u=2),
-        )
-        nc.vector.tensor_copy(
-            woven[1][:].bitcast(I32).rearrange("p (t u) -> p t u", u=2),
-            picked[1][:].bitcast(I32).rearrange("p (u t) -> p t u", u=2),
-        )
-        codes = [keep.tile([P, HALF], U32, name="codes%d" % a, align_bytes=64) for a in range(2)]
-        xscale = [keep.tile([P, HALF], U8, name="xscale%d" % a, align_bytes=64) for a in range(2)]
-        for a in range(2):
-            nc.vector.quantize_mx(out=codes[a][:].bitcast(FP8X4), scales=xscale[a][:], in_=woven[a][:])
+        gather(0, 0, S)
+        gather(1, 0, S)
+        weave(0, 0)
+        weave(0, 1)
+        gather(2, 0, S)
+        for a, b in pieces:
+            gather(3, a, b)
+        weave(1, 0)
+        weave(1, 1)
+        codes = [keep.tile([P, b - a], U32, name="codes%d" % a, align_bytes=64) for a, b in pieces]
+        xscale = [keep.tile([P, b - a], U8, name="xscale%d" % a, align_bytes=64) for a, b in pieces]
+        for i in range(len(pieces)):
+            nc.vector.quantize_mx(out=codes[i][:].bitcast(FP8X4), scales=xscale[i][:], in_=woven[i][:])
 
         rows = {}
 
-        def product(name, b):
+        def product(name, b, groups):
             rows[name, b] = keep.tile([P, S], F32, name="rows_%s%d" % (name, b))
+            for bank_no, members, on_vector in groups:
+                lo, hi = pieces[members[0]][0], pieces[members[-1]][1]
+                bank = psum.tile([P, hi - lo], F32, name="bank%d" % bank_no)
+                for i in members:
+                    nc.tensor.matmul_mx(
+                        out=bank[:, pieces[i][0] - lo : pieces[i][1] - lo],
+                        lhsT=words[name][:, 2 * P * b : 2 * P * (b + 1)].bitcast(FP4X4),
+                        lhsT_scale=scales[name][:, P * b : P * (b + 1)],
+                        rhs=codes[i][:].bitcast(FP8X4),
+                        rhs_scale=xscale[i][:],
+                        start=True,
+                        stop=True,
+                    )
+                if on_vector:
+                    nc.vector.tensor_copy(rows[name, b][:, lo:hi], bank[:])
+                else:
+                    nc.scalar.activation(rows[name, b][:, lo:hi], bank[:], ACT.Copy)
+
+        every = list(range(len(pieces)))
+        product("g", 0, [(0, [0], False), (1, [1], True)])
+        product("s", 0, [(2, [0], False), (3, [1], False)])
+        product("h", 0, [(4, every, False)])
+        product("g", 1, [(5, every, False)])
+        product("s", 1, [(6, every, False)])
+        product("h", 1, [(7, every, False)])
+        acc_bank = [0, 1]
+        u_bank = [[1, 2, 3], [4, 5]]
+
+        def turn(dst, src, start, stop):
             for a in range(2):
-                bank = psum.tile([P, HALF], F32, name="bank")
-                nc.tensor.matmul_mx(
-                    out=bank[:],
-                    lhsT=words[name][:, 2 * P * b : 2 * P * (b + 1)].bitcast(FP4X4),
-                    lhsT_scale=scales[name][:, P * b : P * (b + 1)],
-                    rhs=codes[a][:].bitcast(FP8X4),
-                    rhs_scale=xscale[a][:],
-                    start=True,
-                    stop=True,
+                part = slice(a * P, (a + 1) * P)
+                nc.tensor.matmul(
+                    dst[:, part], lhsT=src[:, part], rhs=ident[:], is_transpose=True,
+                    start=start and a == 0, stop=stop and a == 1,
                 )
-                nc.scalar.activation(rows[name, b][:, a * HALF : (a + 1) * HALF], bank[:], ACT.Copy)
 
         for b in range(2):
-            for name in "ghs":
-                product(name, b)
-
-        for b in range(2):
-            gc = keep.tile([P, V], F32, name="gc%d" % b)
-            sc = keep.tile([P, V], F32, name="sc%d" % b)
+            gc = keep.tile([P, V], F32, name=["gc0", "t0_1"][b])
+            sc = keep.tile([P, V], F32, name=["sc0", "rows_h0"][b])
             nc.vector.tensor_copy(gc[:], rows["g", b][:].indirect(cen_sb[:]))
-            t = [keep.tile([P, V], F32, name="t%d_%d" % (b, d)) for d in range(3)]
-            u = [keep.tile([P, V], F32, name="u%d_%d" % (b, d)) for d in range(3)]
-            r = [keep.tile([P, V], F32, name="r%d_%d" % (b, d)) for d in range(3)]
-            nc.vector.tensor_tensor(t[0][:], rows["h", b][:].indirect(pos_sb[0][:]), gc[:], ALU.mult)
             nc.vector.tensor_copy(sc[:], rows["s", b][:].indirect(cen_sb[:]))
-            nc.vector.tensor_tensor(t[1][:], rows["h", b][:].indirect(pos_sb[1][:]), gc[:], ALU.mult)
-            nc.vector.tensor_tensor(u[0][:], t[0][:], sc[:], ALU.add)
-            nc.scalar.activation(r[0][:], u[0][:], ACT.Relu)
-            nc.vector.tensor_tensor(t[2][:], rows["h", b][:].indirect(pos_sb[2][:]), gc[:], ALU.mult)
-            nc.vector.tensor_tensor(u[1][:], t[1][:], sc[:], ALU.add)
-            nc.vector.tensor_tensor(u[2][:], t[2][:], sc[:], ALU.add)
-            nc.vector.scalar_tensor_tensor(r[1][:], u[1][:], 0.0, r[0][:], ALU.max, ALU.add)
-            nc.vector.scalar_tensor_tensor(r[2][:], u[2][:], 0.0, r[1][:], ALU.max, ALU.add)
-            nc.sync.dma_start(out[P * b : P * (b + 1), :], r[2][:])
+            turned = [3, 1][b]
+            acc = psum.tile([P, V], F32, name="bank%d" % acc_bank[b])
+            for d in range(turned):
+                t = keep.tile([P, V], F32, name="t%d_%d" % (b, d))
+                nc.vector.tensor_tensor(t[:], rows["h", b][:].indirect(pos_sb[d][:]), gc[:], ALU.mult)
+                uT = psum.tile([P, V], F32, name="bank%d" % u_bank[b][d])
+                turn(uT, sc, True, False)
+                turn(uT, t, False, True)
+                rT = keep.tile([P, V], F32, name="r%d_%d" % (b, d))
+                nc.scalar.activation(rT[:], uT[:], ACT.Relu)
+                turn(acc, rT, d == 0, d == turned - 1)
+            if turned == 3:
+                res = keep.tile([P, V], F32, name="res%d" % b)
+                nc.scalar.activation(res[:], acc[:], ACT.Copy)
+                nc.sync.dma_start(out[P * b : P * (b + 1), :], res[:])
+            else:
+                rest = range(turned, 3)
+                t = {d: keep.tile([P, V], F32, name="tl%d_%d" % (b, d)) for d in rest}
+                u = {d: keep.tile([P, V], F32, name="ul%d_%d" % (b, d)) for d in rest}
+                for d in rest:
+                    nc.vector.tensor_tensor(t[d][:], rows["h", b][:].indirect(pos_sb[d][:]), gc[:], ALU.mult)
+                for d in rest:
+                    nc.vector.tensor_tensor(u[d][:], t[d][:], sc[:], ALU.add)
+                parts = [slice(P * a, P * (a + 1)) for a in range(2)]
+                total = [acc[:, part] for part in parts]
+                for d in rest:
+                    for a, part in enumerate(parts):
+                        res = keep.tile([P, P], F32, name="res%d_%d_%d" % (b, d, a))
+                        nc.vector.scalar_tensor_tensor(res[:], u[d][:, part], 0.0, total[a], ALU.max, ALU.add)
+                        total[a] = res[:]
+                for a, part in enumerate(parts):
+                    nc.sync.dma_start(out[P * b : P * (b + 1), part], total[a])

@@ -18,6 +18,12 @@ ALU = mybir.AluOpType
 ACT = mybir.ActivationFunctionType
 
 P = 128
+PACK = 4
+LIST_ROWS = 16
+QUADRANT = 32
+BLOCKS = N // P
+TURNED = 2
+HALVES = [(0, S // 2), (S // 2, S)]
 
 
 def tile_picked_filmg_relu_e_kernel(
@@ -28,150 +34,138 @@ def tile_picked_filmg_relu_e_kernel(
         keep = ctx.enter_context(tc.tile_pool(name="keep", bufs=1))
         psum = ctx.enter_context(tc.psum_pool(name="psum", bufs=1))
 
+        def bank(number, width):
+            return psum.tile([P, width], F32, name="bank%d" % number)
+
         def load_list(name, src):
             tile = keep.tile(list(src.shape), U16, name=name)
             nc.sync.dma_start(tile[:], src)
             return tile
 
-        weights = {"g": (w1_words, w1_scales), "s": (w2_words, w2_scales), "h": (w3_words, w3_scales)}
-        scales = {name: keep.tile([P, N], U8, name="scales_" + name, align_bytes=64) for name in "gsh"}
-        words = {name: keep.tile([P, 2 * N], U8, name="words_" + name, align_bytes=64) for name in "gsh"}
-
-        def load_words(name):
-            nc.sync.dma_start(words[name][:].bitcast(I32), weights[name][0][0].bitcast(I32))
-
-        def load_scales(name, queue):
-            for q in range(4):
-                queue.dma_start(
-                    scales[name][32 * q : 32 * q + 32, :].bitcast(I32),
-                    weights[name][1][0, 4 * q : 4 * q + 4, :].bitcast(I32).unsqueeze(0).to_broadcast([8, 4, N // 4]),
-                )
-
+        x_rows = xT.rearrange("(p j) t -> p j t", j=PACK)
+        planes = [keep.tile([P, T], F32, name="plane%d" % j) for j in range(PACK)]
+        nc.sync.dma_start(planes[0][:], x_rows[:, 0, :])
         offs_sb = load_list("offs_sb", offs)
-        x_rows = xT.rearrange("(p j) t -> p j t", j=4)
-        planes = []
-        for j in range(4):
-            plane = keep.tile([P, T], F32, name="plane%d" % j)
-            nc.sync.dma_start(plane[:], x_rows[:, j, :])
-            planes.append(plane)
+        for j in range(1, PACK):
+            nc.sync.dma_start(planes[j][:], x_rows[:, j, :])
 
-        load_words("g")
-        load_scales("g", nc.sync)
-        load_words("s")
-        load_scales("s", nc.sync)
-        load_words("h")
-        load_scales("h", nc.sync)
+        words, scales = {}, {}
+        for name, w_words, w_scales in (("g", w1_words, w1_scales), ("s", w2_words, w2_scales), ("h", w3_words, w3_scales)):
+            words[name] = keep.tile([P, 2 * N], U8, name="words_" + name, align_bytes=64)
+            scales[name] = keep.tile([P, N], U8, name="scales_" + name, align_bytes=64)
+            nc.sync.dma_start(words[name][:].bitcast(I32), w_words[0].bitcast(I32))
+            for q in range(P // QUADRANT):
+                four_rows = w_scales[0, 4 * q : 4 * q + 4, :].bitcast(I32)
+                nc.sync.dma_start(
+                    scales[name][QUADRANT * q : QUADRANT * (q + 1), :].bitcast(I32),
+                    four_rows.unsqueeze(0).to_broadcast([QUADRANT // 4, 4, N // 4]),
+                )
         cen_sb = load_list("cen_sb", cen)
         pos_sb = [load_list("pos%d_sb" % d, src) for d, src in enumerate((pos1, pos2, pos3))]
 
         ident = keep.tile([P, P], F32)
         make_identity(nc, ident[:])
 
-        pieces = [(0, 256), (256, 512)]
         picked = [keep.tile([P, 2 * S], BF16, name="picked%d" % u) for u in range(2)]
-        woven = [keep.tile([P, 4 * (b - a)], BF16, name="woven%d" % a, align_bytes=64) for a, b in pieces]
+        woven = [keep.tile([P, PACK * (b - a)], BF16, name="woven%d" % a, align_bytes=64) for a, b in HALVES]
 
-        def gather(j, a, b):
+        def gather_plane(j, a, b):
             u, e = divmod(j, 2)
-            nc.vector.tensor_copy(picked[u][:, e * S + a : e * S + b], planes[j][:].indirect(offs_sb[:, a // 16 : b // 16]))
+            entries = offs_sb[:, a // LIST_ROWS : b // LIST_ROWS]
+            nc.vector.tensor_copy(picked[u][:, e * S + a : e * S + b], planes[j][:].indirect(entries))
 
-        def weave(u, i):
-            a, b = pieces[i]
-            dst = woven[i][:].rearrange("p (t j) -> p t j", j=4)[:, :, 2 * u : 2 * u + 2]
-            src = picked[u][:].rearrange("p (e t) -> p t e", e=2)[:, a:b, :]
-            if u == 0:
-                nc.scalar.copy(dst, src)
-            else:
-                nc.vector.tensor_copy(dst, src)
+        def weave(copy, u, i):
+            a, b = HALVES[i]
+            copy(
+                woven[i][:].rearrange("p (t j) -> p t j", j=PACK)[:, :, 2 * u : 2 * u + 2],
+                picked[u][:].rearrange("p (e t) -> p t e", e=2)[:, a:b, :],
+            )
 
-        gather(0, 0, S)
-        gather(1, 0, S)
-        weave(0, 0)
-        weave(0, 1)
-        gather(2, 0, S)
-        for a, b in pieces:
-            gather(3, a, b)
-        weave(1, 0)
-        weave(1, 1)
-        codes = [keep.tile([P, b - a], U32, name="codes%d" % a, align_bytes=64) for a, b in pieces]
-        xscale = [keep.tile([P, b - a], U8, name="xscale%d" % a, align_bytes=64) for a, b in pieces]
-        for i in range(len(pieces)):
-            nc.vector.quantize_mx(out=codes[i][:].bitcast(FP8X4), scales=xscale[i][:], in_=woven[i][:])
+        gather_plane(0, 0, S)
+        gather_plane(1, 0, S)
+        for i in range(len(HALVES)):
+            weave(nc.scalar.copy, 0, i)
+        gather_plane(2, 0, S)
+        for a, b in HALVES:
+            gather_plane(3, a, b)
+        for i in range(len(HALVES)):
+            weave(nc.vector.tensor_copy, 1, i)
 
-        rows = {}
+        codes = [keep.tile([P, b - a], U32, name="codes%d" % a, align_bytes=64) for a, b in HALVES]
+        x_scales = [keep.tile([P, b - a], U8, name="x_scales%d" % a, align_bytes=64) for a, b in HALVES]
+        for i in range(len(HALVES)):
+            nc.vector.quantize_mx(out=codes[i][:].bitcast(FP8X4), scales=x_scales[i][:], in_=woven[i][:])
 
-        def product(name, b, groups):
-            rows[name, b] = keep.tile([P, S], F32, name="rows_%s%d" % (name, b))
-            for bank_no, members, on_vector in groups:
-                lo, hi = pieces[members[0]][0], pieces[members[-1]][1]
-                bank = psum.tile([P, hi - lo], F32, name="bank%d" % bank_no)
-                for i in members:
-                    nc.tensor.matmul_mx(
-                        out=bank[:, pieces[i][0] - lo : pieces[i][1] - lo],
-                        lhsT=words[name][:, 2 * P * b : 2 * P * (b + 1)].bitcast(FP4X4),
-                        lhsT_scale=scales[name][:, P * b : P * (b + 1)],
-                        rhs=codes[i][:].bitcast(FP8X4),
-                        rhs_scale=xscale[i][:],
-                        start=True,
-                        stop=True,
-                    )
-                if on_vector:
-                    nc.vector.tensor_copy(rows[name, b][:, lo:hi], bank[:])
-                else:
-                    nc.scalar.activation(rows[name, b][:, lo:hi], bank[:], ACT.Copy)
+        rows = {
+            (name, blk): keep.tile([P, S], F32, name="rows_%s%d" % (name, blk)) for blk in range(BLOCKS) for name in "gsh"
+        }
 
-        every = list(range(len(pieces)))
-        product("g", 0, [(0, [0], False), (1, [1], True)])
-        product("s", 0, [(2, [0], False), (3, [1], False)])
-        product("h", 0, [(4, every, False)])
-        product("g", 1, [(5, every, False)])
-        product("s", 1, [(6, every, False)])
-        product("h", 1, [(7, every, False)])
-        acc_bank = [0, 1]
-        u_bank = [[1, 2, 3], [4, 5]]
+        def multiply(dst, name, blk, i):
+            nc.tensor.matmul_mx(
+                out=dst,
+                lhsT=words[name][:, 2 * P * blk : 2 * P * (blk + 1)].bitcast(FP4X4),
+                lhsT_scale=scales[name][:, P * blk : P * (blk + 1)],
+                rhs=codes[i][:].bitcast(FP8X4),
+                rhs_scale=x_scales[i][:],
+                start=True,
+                stop=True,
+            )
+
+        def scalar_copy_out(dst, src):
+            nc.scalar.activation(dst, src, ACT.Copy)
+
+        for n, name in enumerate("gsh"):
+            for i, (a, b) in enumerate(HALVES):
+                half = bank(2 * n + i, b - a)
+                multiply(half[:], name, 0, i)
+                copy_out = nc.vector.tensor_copy if (name, i) == ("g", 1) else scalar_copy_out
+                copy_out(rows[name, 0][:, a:b], half[:])
+        for name, number in (("g", 6), ("s", 7), ("h", 0)):
+            whole = bank(number, S)
+            for i, (a, b) in enumerate(HALVES):
+                multiply(whole[:, a:b], name, 1, i)
+            scalar_copy_out(rows[name, 1][:], whole[:])
 
         def turn(dst, src, start, stop):
-            for a in range(2):
-                part = slice(a * P, (a + 1) * P)
+            for a in range(V // P):
+                square = slice(a * P, (a + 1) * P)
                 nc.tensor.matmul(
-                    dst[:, part], lhsT=src[:, part], rhs=ident[:], is_transpose=True,
-                    start=start and a == 0, stop=stop and a == 1,
+                    dst[:, square],
+                    lhsT=src[:, square],
+                    rhs=ident[:],
+                    is_transpose=True,
+                    start=start and a == 0,
+                    stop=stop and a == V // P - 1,
                 )
 
-        for b in range(2):
-            gc = keep.tile([P, V], F32, name=["gc0", "t0_1"][b])
-            sc = keep.tile([P, V], F32, name=["sc0", "rows_h0"][b])
-            nc.vector.tensor_copy(gc[:], rows["g", b][:].indirect(cen_sb[:]))
-            nc.vector.tensor_copy(sc[:], rows["s", b][:].indirect(cen_sb[:]))
-            turned = [3, 1][b]
-            acc = psum.tile([P, V], F32, name="bank%d" % acc_bank[b])
-            for d in range(turned):
-                t = keep.tile([P, V], F32, name="t%d_%d" % (b, d))
-                nc.vector.tensor_tensor(t[:], rows["h", b][:].indirect(pos_sb[d][:]), gc[:], ALU.mult)
-                uT = psum.tile([P, V], F32, name="bank%d" % u_bank[b][d])
-                turn(uT, sc, True, False)
-                turn(uT, t, False, True)
-                rT = keep.tile([P, V], F32, name="r%d_%d" % (b, d))
-                nc.scalar.activation(rT[:], uT[:], ACT.Relu)
-                turn(acc, rT, d == 0, d == turned - 1)
-            if turned == 3:
-                res = keep.tile([P, V], F32, name="res%d" % b)
-                nc.scalar.activation(res[:], acc[:], ACT.Copy)
-                nc.sync.dma_start(out[P * b : P * (b + 1), :], res[:])
-            else:
-                rest = range(turned, 3)
-                t = {d: keep.tile([P, V], F32, name="tl%d_%d" % (b, d)) for d in rest}
-                u = {d: keep.tile([P, V], F32, name="ul%d_%d" % (b, d)) for d in rest}
-                for d in rest:
-                    nc.vector.tensor_tensor(t[d][:], rows["h", b][:].indirect(pos_sb[d][:]), gc[:], ALU.mult)
-                for d in rest:
-                    nc.vector.tensor_tensor(u[d][:], t[d][:], sc[:], ALU.add)
-                parts = [slice(P * a, P * (a + 1)) for a in range(2)]
-                total = [acc[:, part] for part in parts]
-                for d in rest:
-                    for a, part in enumerate(parts):
-                        res = keep.tile([P, P], F32, name="res%d_%d_%d" % (b, d, a))
-                        nc.vector.scalar_tensor_tensor(res[:], u[d][:, part], 0.0, total[a], ALU.max, ALU.add)
-                        total[a] = res[:]
-                for a, part in enumerate(parts):
-                    nc.sync.dma_start(out[P * b : P * (b + 1), part], total[a])
+        def scaled_neighbour(dst, blk, d):
+            nc.vector.tensor_tensor(dst[:], rows["h", blk][:].indirect(pos_sb[d][:]), g_cen[blk][:], ALU.mult)
+
+        g_cen, s_cen, total = [], [], []
+        for blk in range(BLOCKS):
+            g_cen.append(keep.tile([P, V], F32, name="g_cen%d" % blk))
+            s_cen.append(keep.tile([P, V], F32, name="s_cen%d" % blk))
+            nc.vector.tensor_copy(g_cen[blk][:], rows["g", blk][:].indirect(cen_sb[:]))
+            nc.vector.tensor_copy(s_cen[blk][:], rows["s", blk][:].indirect(cen_sb[:]))
+            first_bank = 1 + (TURNED + 1) * blk
+            total.append(bank(first_bank + TURNED, V))
+            for d in range(TURNED):
+                scaled = keep.tile([P, V], F32, name="scaled%d_%d" % (blk, d))
+                scaled_neighbour(scaled, blk, d)
+                shifted_T = bank(first_bank + d, V)
+                turn(shifted_T, s_cen[blk], True, False)
+                turn(shifted_T, scaled, False, True)
+                relu_T = keep.tile([P, V], F32, name="relu_T%d_%d" % (blk, d))
+                nc.scalar.activation(relu_T[:], shifted_T[:], ACT.Relu)
+                turn(total[blk], relu_T, d == 0, d == TURNED - 1)
+
+        last = [keep.tile([P, V], F32, name=name) for name in ("scaled1_0", "scaled_last")]
+        shifted = [keep.tile([P, V], F32, name="shifted%d" % blk) for blk in range(BLOCKS)]
+        for blk in range(BLOCKS):
+            scaled_neighbour(last[blk], blk, TURNED)
+        for blk in range(BLOCKS):
+            nc.vector.tensor_tensor(shifted[blk][:], last[blk][:], s_cen[blk][:], ALU.add)
+        for blk in range(BLOCKS):
+            result = keep.tile([P, V], F32, name="result%d" % blk)
+            nc.vector.scalar_tensor_tensor(result[:], shifted[blk][:], 0.0, total[blk][:], ALU.max, ALU.add)
+            nc.sync.dma_start(out[P * blk : P * (blk + 1), :], result[:])

@@ -49,17 +49,19 @@ def tile_picked_filmg_relu_e_kernel(
         for j in range(1, PACK):
             nc.sync.dma_start(planes[j][:], x_rows[:, j, :])
 
+        weights = (("g", w1_words, w1_scales), ("s", w2_words, w2_scales), ("h", w3_words, w3_scales))
         words, scales = {}, {}
-        for name, w_words, w_scales in (("g", w1_words, w1_scales), ("s", w2_words, w2_scales), ("h", w3_words, w3_scales)):
-            words[name] = keep.tile([P, 2 * N], U8, name="words_" + name, align_bytes=64)
+        for name, w_words, w_scales in weights:
             scales[name] = keep.tile([P, N], U8, name="scales_" + name, align_bytes=64)
+            rows_from_2 = w_scales[0, 2:16, :].bitcast(I32)
+            nc.scalar.dma_start(
+                scales[name][2:P, :].bitcast(I32),
+                rows_from_2.unsqueeze(0).to_broadcast([(P - 2) // 14, 14, N // 4]),
+            )
+        for name, w_words, w_scales in weights:
+            words[name] = keep.tile([P, 2 * N], U8, name="words_" + name, align_bytes=64)
             nc.sync.dma_start(words[name][:].bitcast(I32), w_words[0].bitcast(I32))
-            for q in range(P // QUADRANT):
-                four_rows = w_scales[0, 4 * q : 4 * q + 4, :].bitcast(I32)
-                nc.sync.dma_start(
-                    scales[name][QUADRANT * q : QUADRANT * (q + 1), :].bitcast(I32),
-                    four_rows.unsqueeze(0).to_broadcast([QUADRANT // 4, 4, N // 4]),
-                )
+            nc.sync.dma_start(scales[name][0:2, :].bitcast(I32), w_scales[0, 0:2, :].bitcast(I32))
         cen_sb = load_list("cen_sb", cen)
         pos_sb = [load_list("pos%d_sb" % d, src) for d, src in enumerate((pos1, pos2, pos3))]
 

@@ -24,6 +24,8 @@ QUADRANT = 32
 BLOCKS = N // P
 TURNED = 2
 HALVES = [(0, S // 2), (S // 2, S)]
+QUANTISE_ORDER = (0, 1)
+PLANE_ORDER = (2, 0, 1, 3)
 
 
 def tile_picked_filmg_relu_e_kernel(
@@ -44,9 +46,9 @@ def tile_picked_filmg_relu_e_kernel(
 
         x_rows = xT.rearrange("(p j) t -> p j t", j=PACK)
         planes = [keep.tile([P, T], F32, name="plane%d" % j) for j in range(PACK)]
-        nc.sync.dma_start(planes[0][:], x_rows[:, 0, :])
+        nc.sync.dma_start(planes[PLANE_ORDER[0]][:], x_rows[:, PLANE_ORDER[0], :])
         offs_sb = load_list("offs_sb", offs)
-        for j in range(1, PACK):
+        for j in PLANE_ORDER[1:]:
             nc.sync.dma_start(planes[j][:], x_rows[:, j, :])
 
         weights = (("g", w1_words, w1_scales), ("s", w2_words, w2_scales), ("h", w3_words, w3_scales))
@@ -54,7 +56,7 @@ def tile_picked_filmg_relu_e_kernel(
         for name, w_words, w_scales in weights:
             scales[name] = keep.tile([P, N], U8, name="scales_" + name, align_bytes=64)
             rows_from_2 = w_scales[0, 2:16, :].bitcast(I32)
-            nc.scalar.dma_start(
+            nc.sync.dma_start(
                 scales[name][2:P, :].bitcast(I32),
                 rows_from_2.unsqueeze(0).to_broadcast([(P - 2) // 14, 14, N // 4]),
             )
@@ -68,34 +70,27 @@ def tile_picked_filmg_relu_e_kernel(
         ident = keep.tile([P, P], F32)
         make_identity(nc, ident[:])
 
-        picked = [keep.tile([P, 2 * S], BF16, name="picked%d" % u) for u in range(2)]
         woven = [keep.tile([P, PACK * (b - a)], BF16, name="woven%d" % a, align_bytes=64) for a, b in HALVES]
+        woven_nodes = [w[:].rearrange("p (t j) -> p t j", j=PACK) for w in woven]
+        picked = keep.tile([P, 2 * S], BF16, name="picked")
+        picked_rows = picked[:].rearrange("p (e t) -> p t e", e=2)
 
-        def gather_plane(j, a, b):
-            u, e = divmod(j, 2)
-            entries = offs_sb[:, a // LIST_ROWS : b // LIST_ROWS]
-            nc.vector.tensor_copy(picked[u][:, e * S + a : e * S + b], planes[j][:].indirect(entries))
+        def gather_plane(dst, j, a, b):
+            nc.vector.tensor_copy(dst, planes[j][:].indirect(offs_sb[:, a // LIST_ROWS : b // LIST_ROWS]))
 
-        def weave(copy, u, i):
-            a, b = HALVES[i]
-            copy(
-                woven[i][:].rearrange("p (t j) -> p t j", j=PACK)[:, :, 2 * u : 2 * u + 2],
-                picked[u][:].rearrange("p (e t) -> p t e", e=2)[:, a:b, :],
-            )
-
-        gather_plane(0, 0, S)
-        gather_plane(1, 0, S)
-        for i in range(len(HALVES)):
-            weave(nc.scalar.copy, 0, i)
-        gather_plane(2, 0, S)
-        for a, b in HALVES:
-            gather_plane(3, a, b)
-        for i in range(len(HALVES)):
-            weave(nc.vector.tensor_copy, 1, i)
+        for i, (a, b) in enumerate(HALVES):
+            gather_plane(picked[:, S + a : S + b], 2, a, b)
+            nc.scalar.copy(woven_nodes[i][:, :, 2], picked[:, S + a : S + b])
+        gather_plane(picked[:, 0:S], 0, 0, S)
+        for i, (a, b) in enumerate(HALVES):
+            gather_plane(picked[:, S + a : S + b], 1, a, b)
+            nc.scalar.copy(woven_nodes[i][:, :, 0:2], picked_rows[:, a:b, :])
+        for i, (a, b) in enumerate(HALVES):
+            gather_plane(woven_nodes[i][:, :, 3], 3, a, b)
 
         codes = [keep.tile([P, b - a], U32, name="codes%d" % a, align_bytes=64) for a, b in HALVES]
         x_scales = [keep.tile([P, b - a], U8, name="x_scales%d" % a, align_bytes=64) for a, b in HALVES]
-        for i in range(len(HALVES)):
+        for i in QUANTISE_ORDER:
             nc.vector.quantize_mx(out=codes[i][:].bitcast(FP8X4), scales=x_scales[i][:], in_=woven[i][:])
 
         rows = {
@@ -117,10 +112,11 @@ def tile_picked_filmg_relu_e_kernel(
             nc.scalar.activation(dst, src, ACT.Copy)
 
         for n, name in enumerate("gsh"):
-            for i, (a, b) in enumerate(HALVES):
+            for i in QUANTISE_ORDER:
+                a, b = HALVES[i]
                 half = bank(2 * n + i, b - a)
                 multiply(half[:], name, 0, i)
-                copy_out = nc.vector.tensor_copy if (name, i) == ("g", 1) else scalar_copy_out
+                copy_out = nc.vector.tensor_copy if (name, i) == ("g", QUANTISE_ORDER[-1]) else scalar_copy_out
                 copy_out(rows[name, 0][:, a:b], half[:])
         for name, number in (("g", 6), ("s", 7), ("h", 0)):
             whole = bank(number, S)

@@ -24,7 +24,7 @@ QUADRANT = 32
 BLOCKS = N // P
 TURNED = 2
 HALVES = [(0, S // 2), (S // 2, S)]
-QUANTISE_ORDER = (0, 1)
+PIECES = [(0, S // 2), (S // 2, 3 * S // 4), (3 * S // 4, S)]
 PLANE_ORDER = (2, 0, 1, 3)
 
 
@@ -85,25 +85,31 @@ def tile_picked_filmg_relu_e_kernel(
         for i, (a, b) in enumerate(HALVES):
             gather_plane(picked[:, S + a : S + b], 1, a, b)
             nc.scalar.copy(woven_nodes[i][:, :, 0:2], picked_rows[:, a:b, :])
-        for i, (a, b) in enumerate(HALVES):
-            gather_plane(woven_nodes[i][:, :, 3], 3, a, b)
+        for a, b in PIECES:
+            i, first = divmod(a, S // 2)
+            gather_plane(woven_nodes[i][:, first : first + b - a, 3], 3, a, b)
 
-        codes = [keep.tile([P, b - a], U32, name="codes%d" % a, align_bytes=64) for a, b in HALVES]
-        x_scales = [keep.tile([P, b - a], U8, name="x_scales%d" % a, align_bytes=64) for a, b in HALVES]
-        for i in QUANTISE_ORDER:
-            nc.vector.quantize_mx(out=codes[i][:].bitcast(FP8X4), scales=x_scales[i][:], in_=woven[i][:])
+        codes = keep.tile([P, S], U32, name="codes", align_bytes=64)
+        x_scales = keep.tile([P, S], U8, name="x_scales", align_bytes=64)
+        for a, b in PIECES:
+            i, first = divmod(a, S // 2)
+            nc.vector.quantize_mx(
+                out=codes[:, a:b].bitcast(FP8X4),
+                scales=x_scales[:, a:b],
+                in_=woven[i][:, PACK * first : PACK * (first + b - a)],
+            )
 
         rows = {
             (name, blk): keep.tile([P, S], F32, name="rows_%s%d" % (name, blk)) for blk in range(BLOCKS) for name in "gsh"
         }
 
-        def multiply(dst, name, blk, i):
+        def multiply(dst, name, blk, a, b):
             nc.tensor.matmul_mx(
                 out=dst,
                 lhsT=words[name][:, 2 * P * blk : 2 * P * (blk + 1)].bitcast(FP4X4),
                 lhsT_scale=scales[name][:, P * blk : P * (blk + 1)],
-                rhs=codes[i][:].bitcast(FP8X4),
-                rhs_scale=x_scales[i][:],
+                rhs=codes[:, a:b].bitcast(FP8X4),
+                rhs_scale=x_scales[:, a:b],
                 start=True,
                 stop=True,
             )
@@ -111,21 +117,22 @@ def tile_picked_filmg_relu_e_kernel(
         def scalar_copy_out(dst, src):
             nc.scalar.activation(dst, src, ACT.Copy)
 
-        for n, name in enumerate("gsh"):
-            for i in QUANTISE_ORDER:
-                a, b = HALVES[i]
-                half = bank(2 * n + i, b - a)
-                multiply(half[:], name, 0, i)
-                copy_out = nc.vector.tensor_copy if (name, i) == ("g", QUANTISE_ORDER[-1]) else scalar_copy_out
-                copy_out(rows[name, 0][:, a:b], half[:])
-        for name, number in (("g", 6), ("s", 7), ("h", 0)):
+        number = 0
+        for name, pieces in (("g", PIECES), ("s", HALVES), ("h", HALVES)):
+            for a, b in pieces:
+                piece = bank(number, b - a)
+                number = number + 1
+                multiply(piece[:], name, 0, a, b)
+                copy_out = nc.vector.tensor_copy if name == "g" and a > 0 else scalar_copy_out
+                copy_out(rows[name, 0][:, a:b], piece[:])
+        for name, number in (("g", 7), ("s", 0), ("h", 1)):
             whole = bank(number, S)
-            for i, (a, b) in enumerate(HALVES):
-                multiply(whole[:, a:b], name, 1, i)
+            multiply(whole[:], name, 1, 0, S)
             scalar_copy_out(rows[name, 1][:], whole[:])
 
         def turn(dst, src, start, stop):
-            for a in range(V // P):
+            squares = src.shape[1] // P
+            for a in range(squares):
                 square = slice(a * P, (a + 1) * P)
                 nc.tensor.matmul(
                     dst[:, square],
@@ -133,37 +140,59 @@ def tile_picked_filmg_relu_e_kernel(
                     rhs=ident[:],
                     is_transpose=True,
                     start=start and a == 0,
-                    stop=stop and a == V // P - 1,
+                    stop=stop and a == squares - 1,
                 )
 
-        def scaled_neighbour(dst, blk, d):
-            nc.vector.tensor_tensor(dst[:], rows["h", blk][:].indirect(pos_sb[d][:]), g_cen[blk][:], ALU.mult)
+        def scaled_neighbour(blk, d, a, b):
+            scaled = keep.tile([P, b - a], F32, name="scaled%d_%d_%d" % (blk, d, a))
+            entries = pos_sb[d][:, a // LIST_ROWS : b // LIST_ROWS]
+            nc.vector.tensor_tensor(scaled[:], rows["h", blk][:].indirect(entries), g_cen[blk][:, a:b], ALU.mult)
+            return scaled
 
-        g_cen, s_cen, total = [], [], []
+        g_cen, s_cen, shifted_T, relu_T = {}, {}, {}, {}
+        shifted_banks = {(0, 0): 2, (0, 1): 3, (1, 0): 5, (1, 1): 6, (0, 2): 0}
+
+        def open_shifted(blk, d, width):
+            shifted_T[blk, d] = bank(shifted_banks[blk, d], width)
+            turn(shifted_T[blk, d][:], s_cen[blk][:, 0:width], True, False)
+
+        def turned_neighbour(blk, d, width):
+            turn(shifted_T[blk, d][:], scaled_neighbour(blk, d, 0, width)[:], False, True)
+            relu_T[blk, d] = keep.tile([P, width], F32, name="relu_T%d_%d" % (blk, d))
+            nc.scalar.activation(relu_T[blk, d][:], shifted_T[blk, d][:], ACT.Relu)
+
         for blk in range(BLOCKS):
-            g_cen.append(keep.tile([P, V], F32, name="g_cen%d" % blk))
-            s_cen.append(keep.tile([P, V], F32, name="s_cen%d" % blk))
+            g_cen[blk] = keep.tile([P, V], F32, name="g_cen%d" % blk)
+            s_cen[blk] = keep.tile([P, V], F32, name="s_cen%d" % blk)
             nc.vector.tensor_copy(g_cen[blk][:], rows["g", blk][:].indirect(cen_sb[:]))
             nc.vector.tensor_copy(s_cen[blk][:], rows["s", blk][:].indirect(cen_sb[:]))
-            first_bank = 1 + (TURNED + 1) * blk
-            total.append(bank(first_bank + TURNED, V))
             for d in range(TURNED):
-                scaled = keep.tile([P, V], F32, name="scaled%d_%d" % (blk, d))
-                scaled_neighbour(scaled, blk, d)
-                shifted_T = bank(first_bank + d, V)
-                turn(shifted_T, s_cen[blk], True, False)
-                turn(shifted_T, scaled, False, True)
-                relu_T = keep.tile([P, V], F32, name="relu_T%d_%d" % (blk, d))
-                nc.scalar.activation(relu_T[:], shifted_T[:], ACT.Relu)
-                turn(total[blk], relu_T, d == 0, d == TURNED - 1)
+                open_shifted(blk, d, V)
+            turned_neighbour(blk, 0, V)
+        open_shifted(0, TURNED, P)
+        for blk in (1, 0):
+            turned_neighbour(blk, 1, V)
+        turned_neighbour(0, TURNED, P)
 
-        last = [keep.tile([P, V], F32, name=name) for name in ("scaled1_0", "scaled_last")]
-        shifted = [keep.tile([P, V], F32, name="shifted%d" % blk) for blk in range(BLOCKS)]
-        for blk in range(BLOCKS):
-            scaled_neighbour(last[blk], blk, TURNED)
-        for blk in range(BLOCKS):
-            nc.vector.tensor_tensor(shifted[blk][:], last[blk][:], s_cen[blk][:], ALU.add)
-        for blk in range(BLOCKS):
-            result = keep.tile([P, V], F32, name="result%d" % blk)
-            nc.vector.scalar_tensor_tensor(result[:], shifted[blk][:], 0.0, total[blk][:], ALU.max, ALU.add)
-            nc.sync.dma_start(out[P * blk : P * (blk + 1), :], result[:])
+        total1, total0_first, total0_second = bank(7, V), bank(4, P), bank(1, P)
+        for d in range(TURNED):
+            for blk in ((0, 1), (1, 0))[d]:
+                if blk == 1:
+                    turn(total1[:], relu_T[1, d][:], d == 0, d == TURNED - 1)
+                else:
+                    turn(total0_second[:], relu_T[0, d][:, P:V], d == 0, d == TURNED - 1)
+                    turn(total0_first[:], relu_T[0, d][:, 0:P], d == 0, False)
+        turn(total0_first[:], relu_T[0, TURNED][:], False, True)
+        result0_first = keep.tile([P, P], F32, name="result0_first")
+        scalar_copy_out(result0_first[:], total0_first[:])
+        nc.sync.dma_start(out[0:P, 0:P], result0_first[:])
+
+        left = ((1, 0, V, total1), (0, P, V, total0_second))
+        last = [scaled_neighbour(blk, TURNED, a, b) for blk, a, b, total in left]
+        shifted = [keep.tile([P, b - a], F32, name="shifted%d" % blk) for blk, a, b, total in left]
+        for n, (blk, a, b, total) in enumerate(left):
+            nc.vector.tensor_tensor(shifted[n][:], last[n][:], s_cen[blk][:, a:b], ALU.add)
+        for n, (blk, a, b, total) in enumerate(left):
+            result = keep.tile([P, b - a], F32, name="result%d" % blk)
+            nc.vector.scalar_tensor_tensor(result[:], shifted[n][:], 0.0, total[:], ALU.max, ALU.add)
+            nc.sync.dma_start(out[P * blk : P * (blk + 1), a:b], result[:])

@@ -72,22 +72,26 @@ def tile_picked_filmg_relu_e_kernel(
 
         woven = [keep.tile([P, PACK * (b - a)], BF16, name="woven%d" % a, align_bytes=64) for a, b in HALVES]
         woven_nodes = [w[:].rearrange("p (t j) -> p t j", j=PACK) for w in woven]
-        picked = keep.tile([P, 2 * S], BF16, name="picked")
-        picked_rows = picked[:].rearrange("p (e t) -> p t e", e=2)
+        picked = keep.tile([P, S + S // 2 + T], BF16, name="picked")
+        picked_rows = picked[:, 0 : 2 * S].rearrange("p (e t) -> p t e", e=2)
+        plane2_bf16 = picked[:, S + S // 2 :]
+
+        def entries(a, b):
+            return offs_sb[:, a // LIST_ROWS : b // LIST_ROWS]
 
         def gather_plane(dst, j, a, b):
-            nc.vector.tensor_copy(dst, planes[j][:].indirect(offs_sb[:, a // LIST_ROWS : b // LIST_ROWS]))
+            nc.vector.tensor_copy(dst, planes[j][:].indirect(entries(a, b)))
 
-        for i, (a, b) in enumerate(HALVES):
-            gather_plane(picked[:, S + a : S + b], 2, a, b)
-            nc.scalar.copy(woven_nodes[i][:, :, 2], picked[:, S + a : S + b])
+        gather_plane(picked[:, S : S + S // 2], 2, *HALVES[0])
+        nc.scalar.copy(plane2_bf16, planes[2][:])
+        nc.scalar.copy(woven_nodes[0][:, :, 2], picked[:, S : S + S // 2])
+        nc.scalar.activation(woven_nodes[1][:, :, 2], plane2_bf16.indirect(entries(*HALVES[1])), ACT.Copy)
         gather_plane(picked[:, 0:S], 0, 0, S)
         for i, (a, b) in enumerate(HALVES):
             gather_plane(picked[:, S + a : S + b], 1, a, b)
             nc.scalar.copy(woven_nodes[i][:, :, 0:2], picked_rows[:, a:b, :])
-        for a, b in PIECES:
-            i, first = divmod(a, S // 2)
-            gather_plane(woven_nodes[i][:, first : first + b - a, 3], 3, a, b)
+        for i, (a, b) in enumerate(HALVES):
+            gather_plane(woven_nodes[i][:, :, 3], 3, a, b)
 
         codes = keep.tile([P, S], U32, name="codes", align_bytes=64)
         x_scales = keep.tile([P, S], U8, name="x_scales", align_bytes=64)
@@ -145,8 +149,8 @@ def tile_picked_filmg_relu_e_kernel(
 
         def scaled_neighbour(blk, d, a, b):
             scaled = keep.tile([P, b - a], F32, name="scaled%d_%d_%d" % (blk, d, a))
-            entries = pos_sb[d][:, a // LIST_ROWS : b // LIST_ROWS]
-            nc.vector.tensor_tensor(scaled[:], rows["h", blk][:].indirect(entries), g_cen[blk][:, a:b], ALU.mult)
+            places = pos_sb[d][:, a // LIST_ROWS : b // LIST_ROWS]
+            nc.vector.tensor_tensor(scaled[:], rows["h", blk][:].indirect(places), g_cen[blk][:, a:b], ALU.mult)
             return scaled
 
         g_cen, s_cen, shifted_T, relu_T = {}, {}, {}, {}

@@ -82,9 +82,8 @@ def tile_picked_filmg_relu_e_kernel(
         def gather_plane(dst, j, a, b):
             nc.vector.tensor_copy(dst, planes[j][:].indirect(entries(a, b)))
 
-        gather_plane(picked[:, S : S + S // 2], 2, *HALVES[0])
+        gather_plane(woven_nodes[0][:, :, 2], 2, *HALVES[0])
         nc.scalar.copy(plane2_bf16, planes[2][:])
-        nc.scalar.copy(woven_nodes[0][:, :, 2], picked[:, S : S + S // 2])
         nc.scalar.activation(woven_nodes[1][:, :, 2], plane2_bf16.indirect(entries(*HALVES[1])), ACT.Copy)
         gather_plane(picked[:, 0:S], 0, 0, S)
         for i, (a, b) in enumerate(HALVES):

@@ -134,8 +134,7 @@ def tile_picked_filmg_relu_e_kernel(
             scalar_copy_out(rows[name, 1][:], whole[:])
 
         def turn(dst, src, start, stop):
-            squares = src.shape[1] // P
-            for a in range(squares):
+            for a in range(V // P):
                 square = slice(a * P, (a + 1) * P)
                 nc.tensor.matmul(
                     dst[:, square],
@@ -143,25 +142,19 @@ def tile_picked_filmg_relu_e_kernel(
                     rhs=ident[:],
                     is_transpose=True,
                     start=start and a == 0,
-                    stop=stop and a == squares - 1,
+                    stop=stop and a == V // P - 1,
                 )
 
-        def scaled_neighbour(blk, d, a, b):
-            scaled = keep.tile([P, b - a], F32, name="scaled%d_%d_%d" % (blk, d, a))
-            places = pos_sb[d][:, a // LIST_ROWS : b // LIST_ROWS]
-            nc.vector.tensor_tensor(scaled[:], rows["h", blk][:].indirect(places), g_cen[blk][:, a:b], ALU.mult)
-            return scaled
+        def scaled_neighbour(dst, blk, d):
+            nc.vector.tensor_tensor(dst[:], rows["h", blk][:].indirect(pos_sb[d][:]), g_cen[blk][:], ALU.mult)
 
-        g_cen, s_cen, shifted_T, relu_T = {}, {}, {}, {}
-        shifted_banks = {(0, 0): 2, (0, 1): 3, (1, 0): 5, (1, 1): 6, (0, 2): 0}
+        g_cen, s_cen, shifted_T, relu_T, total = {}, {}, {}, {}, {}
 
-        def open_shifted(blk, d, width):
-            shifted_T[blk, d] = bank(shifted_banks[blk, d], width)
-            turn(shifted_T[blk, d][:], s_cen[blk][:, 0:width], True, False)
-
-        def turned_neighbour(blk, d, width):
-            turn(shifted_T[blk, d][:], scaled_neighbour(blk, d, 0, width)[:], False, True)
-            relu_T[blk, d] = keep.tile([P, width], F32, name="relu_T%d_%d" % (blk, d))
+        def turned_neighbour(blk, d):
+            scaled = keep.tile([P, V], F32, name="scaled%d_%d" % (blk, d))
+            scaled_neighbour(scaled, blk, d)
+            turn(shifted_T[blk, d], scaled, False, True)
+            relu_T[blk, d] = keep.tile([P, V], F32, name="relu_T%d_%d" % (blk, d))
             nc.scalar.activation(relu_T[blk, d][:], shifted_T[blk, d][:], ACT.Relu)
 
         for blk in range(BLOCKS):
@@ -169,33 +162,24 @@ def tile_picked_filmg_relu_e_kernel(
             s_cen[blk] = keep.tile([P, V], F32, name="s_cen%d" % blk)
             nc.vector.tensor_copy(g_cen[blk][:], rows["g", blk][:].indirect(cen_sb[:]))
             nc.vector.tensor_copy(s_cen[blk][:], rows["s", blk][:].indirect(cen_sb[:]))
+            first_bank = 2 + (TURNED + 1) * blk
+            total[blk] = bank(first_bank + TURNED, V)
             for d in range(TURNED):
-                open_shifted(blk, d, V)
-            turned_neighbour(blk, 0, V)
-        open_shifted(0, TURNED, P)
+                shifted_T[blk, d] = bank(first_bank + d, V)
+                turn(shifted_T[blk, d], s_cen[blk], True, False)
+            turned_neighbour(blk, 0)
         for blk in (1, 0):
-            turned_neighbour(blk, 1, V)
-        turned_neighbour(0, TURNED, P)
+            turned_neighbour(blk, 1)
+        for blk, d in ((0, 0), (1, 0), (1, 1), (0, 1)):
+            turn(total[blk], relu_T[blk, d], d == 0, d == TURNED - 1)
 
-        total1, total0_first, total0_second = bank(7, V), bank(4, P), bank(1, P)
-        for d in range(TURNED):
-            for blk in ((0, 1), (1, 0))[d]:
-                if blk == 1:
-                    turn(total1[:], relu_T[1, d][:], d == 0, d == TURNED - 1)
-                else:
-                    turn(total0_second[:], relu_T[0, d][:, P:V], d == 0, d == TURNED - 1)
-                    turn(total0_first[:], relu_T[0, d][:, 0:P], d == 0, False)
-        turn(total0_first[:], relu_T[0, TURNED][:], False, True)
-        result0_first = keep.tile([P, P], F32, name="result0_first")
-        scalar_copy_out(result0_first[:], total0_first[:])
-        nc.sync.dma_start(out[0:P, 0:P], result0_first[:])
-
-        left = ((1, 0, V, total1), (0, P, V, total0_second))
-        last = [scaled_neighbour(blk, TURNED, a, b) for blk, a, b, total in left]
-        shifted = [keep.tile([P, b - a], F32, name="shifted%d" % blk) for blk, a, b, total in left]
-        for n, (blk, a, b, total) in enumerate(left):
-            nc.vector.tensor_tensor(shifted[n][:], last[n][:], s_cen[blk][:, a:b], ALU.add)
-        for n, (blk, a, b, total) in enumerate(left):
-            result = keep.tile([P, b - a], F32, name="result%d" % blk)
-            nc.vector.scalar_tensor_tensor(result[:], shifted[n][:], 0.0, total[:], ALU.max, ALU.add)
-            nc.sync.dma_start(out[P * blk : P * (blk + 1), a:b], result[:])
+        last = {1: keep.tile([P, V], F32, name="scaled_last"), 0: keep.tile([P, V], F32, name="scaled1_1")}
+        shifted = {1: keep.tile([P, V], F32, name="scaled0_1"), 0: keep.tile([P, V], F32, name="relu_T1_1")}
+        for blk in (1, 0):
+            scaled_neighbour(last[blk], blk, TURNED)
+        for blk in (1, 0):
+            nc.vector.tensor_tensor(shifted[blk][:], last[blk][:], s_cen[blk][:], ALU.add)
+        for blk in (1, 0):
+            result = keep.tile([P, V], F32, name="result%d" % blk)
+            nc.vector.scalar_tensor_tensor(result[:], shifted[blk][:], 0.0, total[blk][:], ALU.max, ALU.add)
+            nc.sync.dma_start(out[P * blk : P * (blk + 1), :], result[:])

@@ -173,8 +173,8 @@ def tile_picked_filmg_relu_e_kernel(
         for blk, d in ((0, 0), (1, 0), (1, 1), (0, 1)):
             turn(total[blk], relu_T[blk, d], d == 0, d == TURNED - 1)
 
-        last = {1: keep.tile([P, V], F32, name="scaled_last"), 0: keep.tile([P, V], F32, name="scaled1_1")}
-        shifted = {1: keep.tile([P, V], F32, name="scaled0_1"), 0: keep.tile([P, V], F32, name="relu_T1_1")}
+        last = {blk: keep.tile([P, V], F32, name="last%d" % blk) for blk in range(BLOCKS)}
+        shifted = {blk: keep.tile([P, V], F32, name="shifted%d" % blk) for blk in range(BLOCKS)}
         for blk in (1, 0):
             scaled_neighbour(last[blk], blk, TURNED)
         for blk in (1, 0):

@@ -134,7 +134,8 @@ def tile_picked_filmg_relu_e_kernel(
             scalar_copy_out(rows[name, 1][:], whole[:])
 
         def turn(dst, src, start, stop):
-            for a in range(V // P):
+            squares = src.shape[1] // P
+            for a in range(squares):
                 square = slice(a * P, (a + 1) * P)
                 nc.tensor.matmul(
                     dst[:, square],
@@ -142,44 +143,52 @@ def tile_picked_filmg_relu_e_kernel(
                     rhs=ident[:],
                     is_transpose=True,
                     start=start and a == 0,
-                    stop=stop and a == V // P - 1,
+                    stop=stop and a == squares - 1,
                 )
 
-        def scaled_neighbour(dst, blk, d):
-            nc.vector.tensor_tensor(dst[:], rows["h", blk][:].indirect(pos_sb[d][:]), g_cen[blk][:], ALU.mult)
+        def scaled_neighbour(blk, d):
+            scaled = keep.tile([P, V], F32, name="scaled%d_%d" % (blk, d))
+            nc.vector.tensor_tensor(scaled[:], rows["h", blk][:].indirect(pos_sb[d][:]), g_cen[blk][:], ALU.mult)
+            return scaled
 
-        g_cen, s_cen, shifted_T, relu_T, total = {}, {}, {}, {}, {}
+        whole, squares = [(0, V)], [(0, P), (P, V)]
+        shifted_runs = {(0, 0): whole, (1, 0): whole, (1, 1): whole, (0, 1): squares}
+        shifted_banks = {(0, 0): [2], (1, 0): [5], (1, 1): [6], (0, 1): [3, 0]}
+        total_runs = {0: squares, 1: whole}
+        total_banks = {0: [4, 1], 1: [7]}
+        g_cen, s_cen, shifted_T, relu_T = {}, {}, {}, {}
 
         def turned_neighbour(blk, d):
-            scaled = keep.tile([P, V], F32, name="scaled%d_%d" % (blk, d))
-            scaled_neighbour(scaled, blk, d)
-            turn(shifted_T[blk, d], scaled, False, True)
+            scaled = scaled_neighbour(blk, d)
             relu_T[blk, d] = keep.tile([P, V], F32, name="relu_T%d_%d" % (blk, d))
-            nc.scalar.activation(relu_T[blk, d][:], shifted_T[blk, d][:], ACT.Relu)
+            for (a, b), dst in zip(shifted_runs[blk, d], shifted_T[blk, d]):
+                turn(dst[:], scaled[:, a:b], False, True)
+                nc.scalar.activation(relu_T[blk, d][:, a:b], dst[:], ACT.Relu)
 
         for blk in range(BLOCKS):
             g_cen[blk] = keep.tile([P, V], F32, name="g_cen%d" % blk)
             s_cen[blk] = keep.tile([P, V], F32, name="s_cen%d" % blk)
             nc.vector.tensor_copy(g_cen[blk][:], rows["g", blk][:].indirect(cen_sb[:]))
             nc.vector.tensor_copy(s_cen[blk][:], rows["s", blk][:].indirect(cen_sb[:]))
-            first_bank = 2 + (TURNED + 1) * blk
-            total[blk] = bank(first_bank + TURNED, V)
             for d in range(TURNED):
-                shifted_T[blk, d] = bank(first_bank + d, V)
-                turn(shifted_T[blk, d], s_cen[blk], True, False)
+                shifted_T[blk, d] = []
+                for (a, b), number in zip(shifted_runs[blk, d], shifted_banks[blk, d]):
+                    shifted_T[blk, d].append(bank(number, b - a))
+                    turn(shifted_T[blk, d][-1][:], s_cen[blk][:, a:b], True, False)
             turned_neighbour(blk, 0)
         for blk in (1, 0):
             turned_neighbour(blk, 1)
+        total = {blk: [bank(n, b - a) for (a, b), n in zip(total_runs[blk], total_banks[blk])] for blk in range(BLOCKS)}
         for blk, d in ((0, 0), (1, 0), (1, 1), (0, 1)):
-            turn(total[blk], relu_T[blk, d], d == 0, d == TURNED - 1)
+            for (a, b), dst in zip(total_runs[blk], total[blk]):
+                turn(dst[:], relu_T[blk, d][:, a:b], d == 0, d == TURNED - 1)
 
-        last = {blk: keep.tile([P, V], F32, name="last%d" % blk) for blk in range(BLOCKS)}
+        last = {blk: scaled_neighbour(blk, TURNED) for blk in (1, 0)}
         shifted = {blk: keep.tile([P, V], F32, name="shifted%d" % blk) for blk in range(BLOCKS)}
-        for blk in (1, 0):
-            scaled_neighbour(last[blk], blk, TURNED)
         for blk in (1, 0):
             nc.vector.tensor_tensor(shifted[blk][:], last[blk][:], s_cen[blk][:], ALU.add)
         for blk in (1, 0):
-            result = keep.tile([P, V], F32, name="result%d" % blk)
-            nc.vector.scalar_tensor_tensor(result[:], shifted[blk][:], 0.0, total[blk][:], ALU.max, ALU.add)
-            nc.sync.dma_start(out[P * blk : P * (blk + 1), :], result[:])
+            for (a, b), src in zip(total_runs[blk], total[blk]):
+                result = keep.tile([P, b - a], F32, name="result%d_%d" % (blk, a))
+                nc.vector.scalar_tensor_tensor(result[:], shifted[blk][:, a:b], 0.0, src[:], ALU.max, ALU.add)
+                nc.sync.dma_start(out[P * blk : P * (blk + 1), a:b], result[:])

@@ -21,6 +21,7 @@ P = 128
 PACK = 4
 LIST_ROWS = 16
 QUADRANT = 32
+BANKS = 8
 BLOCKS = N // P
 TURNED = 2
 HALVES = [(0, S // 2), (S // 2, S)]
@@ -120,18 +121,13 @@ def tile_picked_filmg_relu_e_kernel(
         def scalar_copy_out(dst, src):
             nc.scalar.activation(dst, src, ACT.Copy)
 
-        number = 0
-        for name, pieces in (("g", PIECES), ("s", HALVES), ("h", HALVES)):
-            for a, b in pieces:
-                piece = bank(number, b - a)
-                number = number + 1
-                multiply(piece[:], name, 0, a, b)
-                copy_out = nc.vector.tensor_copy if name == "g" and a > 0 else scalar_copy_out
-                copy_out(rows[name, 0][:, a:b], piece[:])
-        for name, number in (("g", 7), ("s", 0), ("h", 1)):
-            whole = bank(number, S)
-            multiply(whole[:], name, 1, 0, S)
-            scalar_copy_out(rows[name, 1][:], whole[:])
+        passes = [(name, blk, a, b) for name in "gsh" for blk in range(BLOCKS)
+                  for a, b in (PIECES if (name, blk) == ("g", 0) else HALVES)]
+        for n, (name, blk, a, b) in enumerate(passes):
+            piece = bank(n % BANKS, b - a)
+            multiply(piece[:], name, blk, a, b)
+            copy_out = nc.vector.tensor_copy if (name, blk) == ("g", 0) and a > 0 else scalar_copy_out
+            copy_out(rows[name, blk][:, a:b], piece[:])
 
         def turn(dst, src, start, stop):
             squares = src.shape[1] // P
@@ -153,9 +149,9 @@ def tile_picked_filmg_relu_e_kernel(
 
         whole, squares = [(0, V)], [(0, P), (P, V)]
         shifted_runs = {(0, 0): whole, (1, 0): whole, (1, 1): whole, (0, 1): squares}
-        shifted_banks = {(0, 0): [2], (1, 0): [5], (1, 1): [6], (0, 1): [3, 0]}
+        shifted_banks = {(0, 0): [5], (0, 1): [6, 7], (1, 0): [0], (1, 1): [1]}
         total_runs = {0: squares, 1: whole}
-        total_banks = {0: [4, 1], 1: [7]}
+        total_banks = {0: [2, 3], 1: [4]}
         g_cen, s_cen, shifted_T, relu_T = {}, {}, {}, {}
 
         def turned_neighbour(blk, d):
@@ -165,11 +161,11 @@ def tile_picked_filmg_relu_e_kernel(
                 turn(dst[:], scaled[:, a:b], False, True)
                 nc.scalar.activation(relu_T[blk, d][:, a:b], dst[:], ACT.Relu)
 
+        for name, centres in (("g", g_cen), ("s", s_cen)):
+            for blk in range(BLOCKS):
+                centres[blk] = keep.tile([P, V], F32, name="%s_cen%d" % (name, blk))
+                nc.vector.tensor_copy(centres[blk][:], rows[name, blk][:].indirect(cen_sb[:]))
         for blk in range(BLOCKS):
-            g_cen[blk] = keep.tile([P, V], F32, name="g_cen%d" % blk)
-            s_cen[blk] = keep.tile([P, V], F32, name="s_cen%d" % blk)
-            nc.vector.tensor_copy(g_cen[blk][:], rows["g", blk][:].indirect(cen_sb[:]))
-            nc.vector.tensor_copy(s_cen[blk][:], rows["s", blk][:].indirect(cen_sb[:]))
             for d in range(TURNED):
                 shifted_T[blk, d] = []
                 for (a, b), number in zip(shifted_runs[blk, d], shifted_banks[blk, d]):

@@ -26,7 +26,8 @@ BLOCKS = N // P
 TURNED = 2
 HALVES = [(0, S // 2), (S // 2, S)]
 PIECES = [(0, S // 2), (S // 2, 3 * S // 4), (3 * S // 4, S)]
-PLANE_ORDER = (2, 0, 1, 3)
+QUARTERS = [(a, a + S // 4) for a in range(0, S, S // 4)]
+PLANE_ORDER = (3, 0, 1, 2)
 
 
 def tile_picked_filmg_relu_e_kernel(
@@ -73,9 +74,9 @@ def tile_picked_filmg_relu_e_kernel(
 
         woven = [keep.tile([P, PACK * (b - a)], BF16, name="woven%d" % a, align_bytes=64) for a, b in HALVES]
         woven_nodes = [w[:].rearrange("p (t j) -> p t j", j=PACK) for w in woven]
-        picked = keep.tile([P, S + S // 2 + T], BF16, name="picked")
-        picked_rows = picked[:, 0 : 2 * S].rearrange("p (e t) -> p t e", e=2)
-        plane2_bf16 = picked[:, S + S // 2 :]
+        picked = keep.tile([P, 3 * S], BF16, name="picked")
+        picked_rows = picked[:].rearrange("p (e t) -> p t e", e=3)
+        plane3_bf16 = keep.tile([P, T], BF16, name="plane3_bf16")
 
         def entries(a, b):
             return offs_sb[:, a // LIST_ROWS : b // LIST_ROWS]
@@ -83,19 +84,23 @@ def tile_picked_filmg_relu_e_kernel(
         def gather_plane(dst, j, a, b):
             nc.vector.tensor_copy(dst, planes[j][:].indirect(entries(a, b)))
 
-        gather_plane(woven_nodes[0][:, :, 2], 2, *HALVES[0])
-        nc.scalar.copy(plane2_bf16, planes[2][:])
-        nc.scalar.activation(woven_nodes[1][:, :, 2], plane2_bf16.indirect(entries(*HALVES[1])), ACT.Copy)
+        half = S // 2
+        gather_plane(woven_nodes[0][:, :, 3], 3, *HALVES[0])
+        nc.scalar.copy(plane3_bf16[:], planes[3][:])
+        nc.scalar.activation(woven_nodes[1][:, :, 3], plane3_bf16[:].indirect(entries(*HALVES[1])), ACT.Copy)
         gather_plane(picked[:, 0:S], 0, 0, S)
-        for i, (a, b) in enumerate(HALVES):
+        for a, b in HALVES:
             gather_plane(picked[:, S + a : S + b], 1, a, b)
-            nc.scalar.copy(woven_nodes[i][:, :, 0:2], picked_rows[:, a:b, :])
-        for i, (a, b) in enumerate(HALVES):
-            gather_plane(woven_nodes[i][:, :, 3], 3, a, b)
+        nc.scalar.copy(woven_nodes[0][:, :, 0:2], picked_rows[:, 0:half, 0:2])
+        for a, b in QUARTERS[2:]:
+            gather_plane(picked[:, 2 * S + a : 2 * S + b], 2, a, b)
+            nc.scalar.copy(woven_nodes[1][:, a - half : b - half, 0:3], picked_rows[:, a:b, :])
+        for a, b in QUARTERS[:2]:
+            gather_plane(woven_nodes[0][:, a:b, 2], 2, a, b)
 
         codes = keep.tile([P, S], U32, name="codes", align_bytes=64)
         x_scales = keep.tile([P, S], U8, name="x_scales", align_bytes=64)
-        for a, b in PIECES:
+        for a, b in QUARTERS:
             i, first = divmod(a, S // 2)
             nc.vector.quantize_mx(
                 out=codes[:, a:b].bitcast(FP8X4),

@@ -25,8 +25,8 @@ BANKS = 8
 BLOCKS = N // P
 TURNED = 2
 HALVES = [(0, S // 2), (S // 2, S)]
-PIECES = [(0, S // 2), (S // 2, 3 * S // 4), (3 * S // 4, S)]
-QUARTERS = [(a, a + S // 4) for a in range(0, S, S // 4)]
+PIECES = [(S // 2, 3 * S // 4), (0, S // 2), (3 * S // 4, S)]
+DIRECT = 224
 PLANE_ORDER = (3, 0, 1, 2)
 
 
@@ -62,7 +62,6 @@ def tile_picked_filmg_relu_e_kernel(
                 scales[name][2:P, :].bitcast(I32),
                 rows_from_2.unsqueeze(0).to_broadcast([(P - 2) // 14, 14, N // 4]),
             )
-        for name, w_words, w_scales in weights:
             words[name] = keep.tile([P, 2 * N], U8, name="words_" + name, align_bytes=64)
             nc.sync.dma_start(words[name][:].bitcast(I32), w_words[0].bitcast(I32))
             nc.sync.dma_start(scales[name][0:2, :].bitcast(I32), w_scales[0, 0:2, :].bitcast(I32))
@@ -72,8 +71,8 @@ def tile_picked_filmg_relu_e_kernel(
         ident = keep.tile([P, P], F32)
         make_identity(nc, ident[:])
 
-        woven = [keep.tile([P, PACK * (b - a)], BF16, name="woven%d" % a, align_bytes=64) for a, b in HALVES]
-        woven_nodes = [w[:].rearrange("p (t j) -> p t j", j=PACK) for w in woven]
+        woven = keep.tile([P, PACK * S], BF16, name="woven", align_bytes=64)
+        woven_nodes = woven[:].rearrange("p (t j) -> p t j", j=PACK)
         picked = keep.tile([P, 3 * S], BF16, name="picked")
         picked_rows = picked[:].rearrange("p (e t) -> p t e", e=3)
         plane3_bf16 = keep.tile([P, T], BF16, name="plane3_bf16")
@@ -84,28 +83,25 @@ def tile_picked_filmg_relu_e_kernel(
         def gather_plane(dst, j, a, b):
             nc.vector.tensor_copy(dst, planes[j][:].indirect(entries(a, b)))
 
-        half = S // 2
-        gather_plane(woven_nodes[0][:, :, 3], 3, *HALVES[0])
+        gather_plane(woven_nodes[:, 0:DIRECT, 3], 3, 0, DIRECT)
         nc.scalar.copy(plane3_bf16[:], planes[3][:])
-        nc.scalar.activation(woven_nodes[1][:, :, 3], plane3_bf16[:].indirect(entries(*HALVES[1])), ACT.Copy)
+        nc.scalar.activation(woven_nodes[:, DIRECT:S, 3], plane3_bf16[:].indirect(entries(DIRECT, S)), ACT.Copy)
         gather_plane(picked[:, 0:S], 0, 0, S)
-        for a, b in HALVES:
+        for a, b in ((0, DIRECT), (DIRECT, S)):
             gather_plane(picked[:, S + a : S + b], 1, a, b)
-        nc.scalar.copy(woven_nodes[0][:, :, 0:2], picked_rows[:, 0:half, 0:2])
-        for a, b in QUARTERS[2:]:
+        nc.scalar.copy(woven_nodes[:, 0:DIRECT, 0:2], picked_rows[:, 0:DIRECT, 0:2])
+        for a, b in ((DIRECT, 3 * S // 4), (3 * S // 4, S)):
             gather_plane(picked[:, 2 * S + a : 2 * S + b], 2, a, b)
-            nc.scalar.copy(woven_nodes[1][:, a - half : b - half, 0:3], picked_rows[:, a:b, :])
-        for a, b in QUARTERS[:2]:
-            gather_plane(woven_nodes[0][:, a:b, 2], 2, a, b)
+            nc.scalar.copy(woven_nodes[:, a:b, 0:3], picked_rows[:, a:b, :])
+        gather_plane(woven_nodes[:, 0:DIRECT, 2], 2, 0, DIRECT)
 
         codes = keep.tile([P, S], U32, name="codes", align_bytes=64)
         x_scales = keep.tile([P, S], U8, name="x_scales", align_bytes=64)
-        for a, b in QUARTERS:
-            i, first = divmod(a, S // 2)
+        for a, b in PIECES:
             nc.vector.quantize_mx(
                 out=codes[:, a:b].bitcast(FP8X4),
                 scales=x_scales[:, a:b],
-                in_=woven[i][:, PACK * first : PACK * (first + b - a)],
+                in_=woven[:, PACK * a : PACK * b],
             )
 
         rows = {
@@ -131,7 +127,7 @@ def tile_picked_filmg_relu_e_kernel(
         for n, (name, blk, a, b) in enumerate(passes):
             piece = bank(n % BANKS, b - a)
             multiply(piece[:], name, blk, a, b)
-            copy_out = nc.vector.tensor_copy if (name, blk) == ("g", 0) and a > 0 else scalar_copy_out
+            copy_out = nc.vector.tensor_copy if (name, blk) == ("g", 0) and b < S else scalar_copy_out
             copy_out(rows[name, blk][:, a:b], piece[:])
 
         def turn(dst, src, start, stop):

@@ -27,6 +27,7 @@ TURNED = 2
 HALVES = [(0, S // 2), (S // 2, S)]
 PIECES = [(S // 2, 3 * S // 4), (0, S // 2), (3 * S // 4, S)]
 DIRECT = 224
+LAST_PIECES = [(0, S // 2), (S // 2, 3 * S // 4), (3 * S // 4, S)]
 PLANE_ORDER = (3, 0, 1, 2)
 
 
@@ -57,16 +58,27 @@ def tile_picked_filmg_relu_e_kernel(
         words, scales = {}, {}
         for name, w_words, w_scales in weights:
             scales[name] = keep.tile([P, N], U8, name="scales_" + name, align_bytes=64)
+            words[name] = keep.tile([P, 2 * N], U8, name="words_" + name, align_bytes=64)
+            nc.scalar.dma_start(scales[name][0:2, :].bitcast(I32), w_scales[0, 0:2, :].bitcast(I32))
+
+        def load_scales(name, w_words, w_scales):
             rows_from_2 = w_scales[0, 2:16, :].bitcast(I32)
             nc.sync.dma_start(
                 scales[name][2:P, :].bitcast(I32),
                 rows_from_2.unsqueeze(0).to_broadcast([(P - 2) // 14, 14, N // 4]),
             )
-            words[name] = keep.tile([P, 2 * N], U8, name="words_" + name, align_bytes=64)
+
+        def load_words(name, w_words, w_scales):
             nc.sync.dma_start(words[name][:].bitcast(I32), w_words[0].bitcast(I32))
-            nc.sync.dma_start(scales[name][0:2, :].bitcast(I32), w_scales[0, 0:2, :].bitcast(I32))
+
+        for load in (load_scales, load_words):
+            for weight in weights[:2]:
+                load(*weight)
         cen_sb = load_list("cen_sb", cen)
-        pos_sb = [load_list("pos%d_sb" % d, src) for d, src in enumerate((pos1, pos2, pos3))]
+        pos_sb = [load_list("pos0_sb", pos1), load_list("pos1_sb", pos2)]
+        load_scales(*weights[2])
+        load_words(*weights[2])
+        pos_sb.append(load_list("pos2_sb", pos3))
 
         ident = keep.tile([P, P], F32)
         make_identity(nc, ident[:])
@@ -123,7 +135,7 @@ def tile_picked_filmg_relu_e_kernel(
             nc.scalar.activation(dst, src, ACT.Copy)
 
         passes = [(name, blk, a, b) for name in "gsh" for blk in range(BLOCKS)
-                  for a, b in (PIECES if (name, blk) == ("g", 0) else HALVES)]
+                  for a, b in {("g", 0): PIECES, ("h", 1): LAST_PIECES}.get((name, blk), HALVES)]
         for n, (name, blk, a, b) in enumerate(passes):
             piece = bank(n % BANKS, b - a)
             multiply(piece[:], name, blk, a, b)
@@ -143,20 +155,19 @@ def tile_picked_filmg_relu_e_kernel(
                     stop=stop and a == squares - 1,
                 )
 
-        def scaled_neighbour(blk, d):
-            scaled = keep.tile([P, V], F32, name="scaled%d_%d" % (blk, d))
-            nc.vector.tensor_tensor(scaled[:], rows["h", blk][:].indirect(pos_sb[d][:]), g_cen[blk][:], ALU.mult)
-            return scaled
+        def scale_neighbour(dst, blk, d):
+            nc.vector.tensor_tensor(dst, rows["h", blk][:].indirect(pos_sb[d][:]), g_cen[blk][:], ALU.mult)
 
         whole, squares = [(0, V)], [(0, P), (P, V)]
-        shifted_runs = {(0, 0): whole, (1, 0): whole, (1, 1): whole, (0, 1): squares}
-        shifted_banks = {(0, 0): [5], (0, 1): [6, 7], (1, 0): [0], (1, 1): [1]}
-        total_runs = {0: squares, 1: whole}
-        total_banks = {0: [2, 3], 1: [4]}
+        shifted_runs = {(0, 0): whole, (0, 1): whole, (1, 0): whole, (1, 1): squares}
+        shifted_banks = {(0, 0): [1], (0, 1): [2], (1, 0): [3], (1, 1): [4, 5]}
+        total_runs = {0: whole, 1: squares}
+        total_banks = {0: [6], 1: [7, 0]}
         g_cen, s_cen, shifted_T, relu_T = {}, {}, {}, {}
 
         def turned_neighbour(blk, d):
-            scaled = scaled_neighbour(blk, d)
+            scaled = keep.tile([P, V], F32, name="scaled%d_%d" % (blk, d))
+            scale_neighbour(scaled[:], blk, d)
             relu_T[blk, d] = keep.tile([P, V], F32, name="relu_T%d_%d" % (blk, d))
             for (a, b), dst in zip(shifted_runs[blk, d], shifted_T[blk, d]):
                 turn(dst[:], scaled[:, a:b], False, True)
@@ -172,19 +183,20 @@ def tile_picked_filmg_relu_e_kernel(
                 for (a, b), number in zip(shifted_runs[blk, d], shifted_banks[blk, d]):
                     shifted_T[blk, d].append(bank(number, b - a))
                     turn(shifted_T[blk, d][-1][:], s_cen[blk][:, a:b], True, False)
-            turned_neighbour(blk, 0)
-        for blk in (1, 0):
-            turned_neighbour(blk, 1)
+            for d in range(TURNED):
+                turned_neighbour(blk, d)
         total = {blk: [bank(n, b - a) for (a, b), n in zip(total_runs[blk], total_banks[blk])] for blk in range(BLOCKS)}
-        for blk, d in ((0, 0), (1, 0), (1, 1), (0, 1)):
+        for blk, d in ((0, 0), (0, 1), (1, 0), (1, 1)):
             for (a, b), dst in zip(total_runs[blk], total[blk]):
                 turn(dst[:], relu_T[blk, d][:, a:b], d == 0, d == TURNED - 1)
 
-        last = {blk: scaled_neighbour(blk, TURNED) for blk in (1, 0)}
+        last = keep.tile([P, BLOCKS * V], F32, name="scaled0_1")
+        for blk in range(BLOCKS):
+            scale_neighbour(last[:, blk * V : (blk + 1) * V], blk, TURNED)
         shifted = {blk: keep.tile([P, V], F32, name="shifted%d" % blk) for blk in range(BLOCKS)}
-        for blk in (1, 0):
-            nc.vector.tensor_tensor(shifted[blk][:], last[blk][:], s_cen[blk][:], ALU.add)
-        for blk in (1, 0):
+        for blk in range(BLOCKS):
+            nc.vector.tensor_tensor(shifted[blk][:], last[:, blk * V : (blk + 1) * V], s_cen[blk][:], ALU.add)
+        for blk in range(BLOCKS):
             for (a, b), src in zip(total_runs[blk], total[blk]):
                 result = keep.tile([P, b - a], F32, name="result%d_%d" % (blk, a))
                 nc.vector.scalar_tensor_tensor(result[:], shifted[blk][:, a:b], 0.0, src[:], ALU.max, ALU.add)

@@ -25,8 +25,8 @@ BANKS = 8
 BLOCKS = N // P
 TURNED = 2
 HALVES = [(0, S // 2), (S // 2, S)]
-PIECES = [(S // 2, 3 * S // 4), (0, S // 2), (3 * S // 4, S)]
-DIRECT = 224
+PIECES = [(a, a + S // 4) for a in range(0, S, S // 4)]
+DIRECT = 256
 LAST_PIECES = [(0, S // 2), (S // 2, 3 * S // 4), (3 * S // 4, S)]
 PLANE_ORDER = (3, 0, 1, 2)
 
@@ -105,7 +105,8 @@ def tile_picked_filmg_relu_e_kernel(
         for a, b in ((DIRECT, 3 * S // 4), (3 * S // 4, S)):
             gather_plane(picked[:, 2 * S + a : 2 * S + b], 2, a, b)
             nc.scalar.copy(woven_nodes[:, a:b, 0:3], picked_rows[:, a:b, :])
-        gather_plane(woven_nodes[:, 0:DIRECT, 2], 2, 0, DIRECT)
+        for a, b in ((0, S // 4), (S // 4, DIRECT)):
+            gather_plane(woven_nodes[:, a:b, 2], 2, a, b)
 
         codes = keep.tile([P, S], U32, name="codes", align_bytes=64)
         x_scales = keep.tile([P, S], U8, name="x_scales", align_bytes=64)
@@ -160,9 +161,9 @@ def tile_picked_filmg_relu_e_kernel(
 
         whole, squares = [(0, V)], [(0, P), (P, V)]
         shifted_runs = {(0, 0): whole, (0, 1): whole, (1, 0): whole, (1, 1): squares}
-        shifted_banks = {(0, 0): [1], (0, 1): [2], (1, 0): [3], (1, 1): [4, 5]}
+        shifted_banks = {(0, 0): [2], (0, 1): [3], (1, 0): [4], (1, 1): [5, 6]}
         total_runs = {0: whole, 1: squares}
-        total_banks = {0: [6], 1: [7, 0]}
+        total_banks = {0: [7], 1: [0, 1]}
         g_cen, s_cen, shifted_T, relu_T = {}, {}, {}, {}
 
         def turned_neighbour(blk, d):

@@ -28,7 +28,8 @@ HALVES = [(0, S // 2), (S // 2, S)]
 PIECES = [(a, a + S // 4) for a in range(0, S, S // 4)]
 DIRECT = 256
 LAST_PIECES = [(0, S // 2), (S // 2, 3 * S // 4), (3 * S // 4, S)]
-PLANE_ORDER = (3, 0, 1, 2)
+VECTOR_CAST = 384
+PLANE_ORDER = (0, 3, 1, 2)
 
 
 def tile_picked_filmg_relu_e_kernel(
@@ -80,8 +81,11 @@ def tile_picked_filmg_relu_e_kernel(
         load_words(*weights[2])
         pos_sb.append(load_list("pos2_sb", pos3))
 
+        zero = keep.tile([P, 1], F32)
+        nc.vector.memset(zero[:], 0.0)
         ident = keep.tile([P, P], F32)
-        make_identity(nc, ident[:])
+        nc.scalar.activation(ident[:], zero[:].to_broadcast([P, P]), ACT.Copy)
+        make_identity(nc, ident[:], nomemset=True)
 
         woven = keep.tile([P, PACK * S], BF16, name="woven", align_bytes=64)
         woven_nodes = woven[:].rearrange("p (t j) -> p t j", j=PACK)
@@ -95,10 +99,11 @@ def tile_picked_filmg_relu_e_kernel(
         def gather_plane(dst, j, a, b):
             nc.vector.tensor_copy(dst, planes[j][:].indirect(entries(a, b)))
 
-        gather_plane(woven_nodes[:, 0:DIRECT, 3], 3, 0, DIRECT)
-        nc.scalar.copy(plane3_bf16[:], planes[3][:])
-        nc.scalar.activation(woven_nodes[:, DIRECT:S, 3], plane3_bf16[:].indirect(entries(DIRECT, S)), ACT.Copy)
         gather_plane(picked[:, 0:S], 0, 0, S)
+        nc.vector.tensor_copy(plane3_bf16[:, 0:VECTOR_CAST], planes[3][:, 0:VECTOR_CAST])
+        nc.scalar.copy(plane3_bf16[:, VECTOR_CAST:T], planes[3][:, VECTOR_CAST:T])
+        gather_plane(woven_nodes[:, 0:DIRECT, 3], 3, 0, DIRECT)
+        nc.scalar.activation(woven_nodes[:, DIRECT:S, 3], plane3_bf16[:].indirect(entries(DIRECT, S)), ACT.Copy)
         for a, b in ((0, DIRECT), (DIRECT, S)):
             gather_plane(picked[:, S + a : S + b], 1, a, b)
         nc.scalar.copy(woven_nodes[:, 0:DIRECT, 0:2], picked_rows[:, 0:DIRECT, 0:2])

@@ -20,16 +20,12 @@ ACT = mybir.ActivationFunctionType
 P = 128
 PACK = 4
 LIST_ROWS = 16
-QUADRANT = 32
-BANKS = 8
 BLOCKS = N // P
 TURNED = 2
-HALVES = [(0, S // 2), (S // 2, S)]
-PIECES = [(a, a + S // 4) for a in range(0, S, S // 4)]
-DIRECT = 256
-LAST_PIECES = [(0, S // 2), (S // 2, 3 * S // 4), (3 * S // 4, S)]
-VECTOR_CAST = 384
-PLANE_ORDER = (0, 3, 1, 2)
+HALF = S // 2
+QUARTER = S // 4
+HALVES = [(0, HALF), (HALF, S)]
+QUARTERS = [(a * QUARTER, (a + 1) * QUARTER) for a in (0, 2, 1, 3)]
 
 
 def tile_picked_filmg_relu_e_kernel(
@@ -50,36 +46,33 @@ def tile_picked_filmg_relu_e_kernel(
 
         x_rows = xT.rearrange("(p j) t -> p j t", j=PACK)
         planes = [keep.tile([P, T], F32, name="plane%d" % j) for j in range(PACK)]
-        nc.sync.dma_start(planes[PLANE_ORDER[0]][:], x_rows[:, PLANE_ORDER[0], :])
+        nc.sync.dma_start(planes[0][:], x_rows[:, 0, :])
         offs_sb = load_list("offs_sb", offs)
-        for j in PLANE_ORDER[1:]:
+        for j in range(1, PACK):
             nc.sync.dma_start(planes[j][:], x_rows[:, j, :])
+        cen_sb = load_list("cen_sb", cen)
+        pos_sb = [load_list("pos%d_sb" % d, src) for d, src in enumerate((pos1, pos2, pos3))]
 
-        weights = (("g", w1_words, w1_scales), ("s", w2_words, w2_scales), ("h", w3_words, w3_scales))
+        weights = {"g": (w1_words, w1_scales), "s": (w2_words, w2_scales), "h": (w3_words, w3_scales)}
         words, scales = {}, {}
-        for name, w_words, w_scales in weights:
+        for name in "ghs":
             scales[name] = keep.tile([P, N], U8, name="scales_" + name, align_bytes=64)
             words[name] = keep.tile([P, 2 * N], U8, name="words_" + name, align_bytes=64)
-            nc.scalar.dma_start(scales[name][0:2, :].bitcast(I32), w_scales[0, 0:2, :].bitcast(I32))
+            nc.gpsimd.dma_start(scales[name][0:2, :].bitcast(I32), weights[name][1][0, 0:2, :].bitcast(I32))
 
-        def load_scales(name, w_words, w_scales):
-            rows_from_2 = w_scales[0, 2:16, :].bitcast(I32)
+        def load_scales(name):
+            rows_from_2 = weights[name][1][0, 2:16, :].bitcast(I32)
             nc.sync.dma_start(
                 scales[name][2:P, :].bitcast(I32),
                 rows_from_2.unsqueeze(0).to_broadcast([(P - 2) // 14, 14, N // 4]),
             )
 
-        def load_words(name, w_words, w_scales):
-            nc.sync.dma_start(words[name][:].bitcast(I32), w_words[0].bitcast(I32))
+        def load_words(name):
+            nc.sync.dma_start(words[name][:].bitcast(I32), weights[name][0][0].bitcast(I32))
 
-        for load in (load_scales, load_words):
-            for weight in weights[:2]:
-                load(*weight)
-        cen_sb = load_list("cen_sb", cen)
-        pos_sb = [load_list("pos0_sb", pos1), load_list("pos1_sb", pos2)]
-        load_scales(*weights[2])
-        load_words(*weights[2])
-        pos_sb.append(load_list("pos2_sb", pos3))
+        for name in "ghs":
+            load_scales(name)
+            load_words(name)
 
         zero = keep.tile([P, 1], F32)
         nc.vector.memset(zero[:], 0.0)
@@ -87,48 +80,43 @@ def tile_picked_filmg_relu_e_kernel(
         nc.scalar.activation(ident[:], zero[:].to_broadcast([P, P]), ACT.Copy)
         make_identity(nc, ident[:], nomemset=True)
 
-        woven = keep.tile([P, PACK * S], BF16, name="woven", align_bytes=64)
-        woven_nodes = woven[:].rearrange("p (t j) -> p t j", j=PACK)
-        picked = keep.tile([P, 3 * S], BF16, name="picked")
-        picked_rows = picked[:].rearrange("p (e t) -> p t e", e=3)
-        plane3_bf16 = keep.tile([P, T], BF16, name="plane3_bf16")
+        woven = [keep.tile([P, PACK * HALF], BF16, name="woven%d" % half, align_bytes=64) for half in range(2)]
+        woven_nodes = [tile[:].rearrange("p (t j) -> p t j", j=PACK) for tile in woven]
+        picked = keep.tile([P, PACK * HALF], BF16, name="picked")
+        picked_nodes = picked[:].rearrange("p (j t) -> p t j", j=PACK)
 
-        def entries(a, b):
-            return offs_sb[:, a // LIST_ROWS : b // LIST_ROWS]
+        def plane_at(j, a, b):
+            return planes[j][:].indirect(offs_sb[:, a // LIST_ROWS : b // LIST_ROWS])
 
-        def gather_plane(dst, j, a, b):
-            nc.vector.tensor_copy(dst, planes[j][:].indirect(entries(a, b)))
-
-        gather_plane(picked[:, 0:S], 0, 0, S)
-        nc.vector.tensor_copy(plane3_bf16[:, 0:VECTOR_CAST], planes[3][:, 0:VECTOR_CAST])
-        nc.scalar.copy(plane3_bf16[:, VECTOR_CAST:T], planes[3][:, VECTOR_CAST:T])
-        gather_plane(woven_nodes[:, 0:DIRECT, 3], 3, 0, DIRECT)
-        nc.scalar.activation(woven_nodes[:, DIRECT:S, 3], plane3_bf16[:].indirect(entries(DIRECT, S)), ACT.Copy)
-        for a, b in ((0, DIRECT), (DIRECT, S)):
-            gather_plane(picked[:, S + a : S + b], 1, a, b)
-        nc.scalar.copy(woven_nodes[:, 0:DIRECT, 0:2], picked_rows[:, 0:DIRECT, 0:2])
-        for a, b in ((DIRECT, 3 * S // 4), (3 * S // 4, S)):
-            gather_plane(picked[:, 2 * S + a : 2 * S + b], 2, a, b)
-            nc.scalar.copy(woven_nodes[:, a:b, 0:3], picked_rows[:, a:b, :])
-        for a, b in ((0, S // 4), (S // 4, DIRECT)):
-            gather_plane(woven_nodes[:, a:b, 2], 2, a, b)
+        for j in range(PACK):
+            runs = [(0, QUARTER), (QUARTER, HALF)] if j == PACK - 1 else [(0, HALF)]
+            for a, b in runs:
+                nc.vector.tensor_copy(woven_nodes[0][:, a:b, j], plane_at(j, a, b))
+                nc.scalar.activation(picked[:, j * HALF + a : j * HALF + b], plane_at(j, HALF + a, HALF + b), ACT.Copy)
+                if j % 2:
+                    nc.scalar.copy(woven_nodes[1][:, a:b, j - 1 : j + 1], picked_nodes[:, a:b, j - 1 : j + 1])
 
         codes = keep.tile([P, S], U32, name="codes", align_bytes=64)
         x_scales = keep.tile([P, S], U8, name="x_scales", align_bytes=64)
-        for a, b in PIECES:
+        for a, b in QUARTERS:
             nc.vector.quantize_mx(
                 out=codes[:, a:b].bitcast(FP8X4),
                 scales=x_scales[:, a:b],
-                in_=woven[:, PACK * a : PACK * b],
+                in_=woven[a // HALF][:, PACK * (a % HALF) : PACK * (a % HALF + QUARTER)],
             )
 
         rows = {
             (name, blk): keep.tile([P, S], F32, name="rows_%s%d" % (name, blk)) for blk in range(BLOCKS) for name in "gsh"
         }
 
-        def multiply(dst, name, blk, a, b):
+        def scalar_copy(dst, src):
+            nc.scalar.activation(dst, src, ACT.Copy)
+
+        def product(name, blk, run, number, copy_out):
+            a, b = run
+            piece = bank(number, b - a)
             nc.tensor.matmul_mx(
-                out=dst,
+                out=piece[:],
                 lhsT=words[name][:, 2 * P * blk : 2 * P * (blk + 1)].bitcast(FP4X4),
                 lhsT_scale=scales[name][:, P * blk : P * (blk + 1)],
                 rhs=codes[:, a:b].bitcast(FP8X4),
@@ -136,18 +124,29 @@ def tile_picked_filmg_relu_e_kernel(
                 start=True,
                 stop=True,
             )
-
-        def scalar_copy_out(dst, src):
-            nc.scalar.activation(dst, src, ACT.Copy)
-
-        passes = [(name, blk, a, b) for name in "gsh" for blk in range(BLOCKS)
-                  for a, b in {("g", 0): PIECES, ("h", 1): LAST_PIECES}.get((name, blk), HALVES)]
-        for n, (name, blk, a, b) in enumerate(passes):
-            piece = bank(n % BANKS, b - a)
-            multiply(piece[:], name, blk, a, b)
-            copy_out = nc.vector.tensor_copy if (name, blk) == ("g", 0) and b < S else scalar_copy_out
             copy_out(rows[name, blk][:, a:b], piece[:])
 
+        def centre(name, blk, copy):
+            tile = keep.tile([P, V], F32, name="%s_cen%d" % (name, blk))
+            copy(tile[:], rows[name, blk][:].indirect(cen_sb[:]))
+            return tile
+
+        on_v, on_s = nc.vector.tensor_copy, scalar_copy
+        g_cen, s_cen = {}, {}
+        for n, run in enumerate(QUARTERS):
+            product("g", 0, run, 2 * n, on_s)
+            product("g", 1, run, 2 * n + 1, on_v)
+        g_cen[0] = centre("g", 0, on_s)
+        g_cen[1] = centre("g", 1, on_v)
+        product("h", 0, HALVES[0], 0, on_s)
+        product("h", 0, HALVES[1], 1, on_v)
+        product("h", 1, HALVES[0], 2, on_s)
+        product("h", 1, HALVES[1], 3, on_s)
+        for blk in range(BLOCKS):
+            for half in range(2):
+                product("s", blk, HALVES[half], 4 + 2 * blk + half, on_s)
+        for blk in range(BLOCKS):
+            s_cen[blk] = centre("s", blk, on_s)
         def turn(dst, src, start, stop):
             squares = src.shape[1] // P
             for a in range(squares):
@@ -161,49 +160,37 @@ def tile_picked_filmg_relu_e_kernel(
                     stop=stop and a == squares - 1,
                 )
 
-        def scale_neighbour(dst, blk, d):
-            nc.vector.tensor_tensor(dst, rows["h", blk][:].indirect(pos_sb[d][:]), g_cen[blk][:], ALU.mult)
+        def scaled_neighbour(blk, d):
+            tile = keep.tile([P, V], F32, name="scaled%d_%d" % (blk, d))
+            nc.vector.tensor_tensor(tile[:], rows["h", blk][:].indirect(pos_sb[d][:]), g_cen[blk][:], ALU.mult)
+            return tile
 
-        whole, squares = [(0, V)], [(0, P), (P, V)]
-        shifted_runs = {(0, 0): whole, (0, 1): whole, (1, 0): whole, (1, 1): squares}
-        shifted_banks = {(0, 0): [2], (0, 1): [3], (1, 0): [4], (1, 1): [5, 6]}
-        total_runs = {0: whole, 1: squares}
-        total_banks = {0: [7], 1: [0, 1]}
-        g_cen, s_cen, shifted_T, relu_T = {}, {}, {}, {}
-
-        def turned_neighbour(blk, d):
-            scaled = keep.tile([P, V], F32, name="scaled%d_%d" % (blk, d))
-            scale_neighbour(scaled[:], blk, d)
-            relu_T[blk, d] = keep.tile([P, V], F32, name="relu_T%d_%d" % (blk, d))
-            for (a, b), dst in zip(shifted_runs[blk, d], shifted_T[blk, d]):
-                turn(dst[:], scaled[:, a:b], False, True)
-                nc.scalar.activation(relu_T[blk, d][:, a:b], dst[:], ACT.Relu)
-
-        for name, centres in (("g", g_cen), ("s", s_cen)):
-            for blk in range(BLOCKS):
-                centres[blk] = keep.tile([P, V], F32, name="%s_cen%d" % (name, blk))
-                nc.vector.tensor_copy(centres[blk][:], rows[name, blk][:].indirect(cen_sb[:]))
+        shifted_banks = {(0, 0): 4, (0, 1): 5, (1, 0): 6, (1, 1): 7}
+        total_runs = {0: [(0, V, 0)], 1: [(0, P, 1), (P, V, 2)]}
+        scaled, shifted_T, relu_T = {}, {}, {}
         for blk in range(BLOCKS):
             for d in range(TURNED):
-                shifted_T[blk, d] = []
-                for (a, b), number in zip(shifted_runs[blk, d], shifted_banks[blk, d]):
-                    shifted_T[blk, d].append(bank(number, b - a))
-                    turn(shifted_T[blk, d][-1][:], s_cen[blk][:, a:b], True, False)
-            for d in range(TURNED):
-                turned_neighbour(blk, d)
-        total = {blk: [bank(n, b - a) for (a, b), n in zip(total_runs[blk], total_banks[blk])] for blk in range(BLOCKS)}
-        for blk, d in ((0, 0), (0, 1), (1, 0), (1, 1)):
-            for (a, b), dst in zip(total_runs[blk], total[blk]):
-                turn(dst[:], relu_T[blk, d][:, a:b], d == 0, d == TURNED - 1)
-
-        last = keep.tile([P, BLOCKS * V], F32, name="scaled0_1")
+                scaled[blk, d] = scaled_neighbour(blk, d)
+                shifted_T[blk, d] = bank(shifted_banks[blk, d], V)
+                turn(shifted_T[blk, d][:], scaled[blk, d][:], True, False)
         for blk in range(BLOCKS):
-            scale_neighbour(last[:, blk * V : (blk + 1) * V], blk, TURNED)
+            scaled[blk, TURNED] = scaled_neighbour(blk, TURNED)
+        for blk in range(BLOCKS):
+            for d in range(TURNED):
+                turn(shifted_T[blk, d][:], s_cen[blk][:], False, True)
+                relu_T[blk, d] = keep.tile([P, V], F32, name="relu_T%d_%d" % (blk, d))
+                nc.scalar.activation(relu_T[blk, d][:], shifted_T[blk, d][:], ACT.Relu)
+        total = {(blk, a): bank(number, b - a) for blk in range(BLOCKS) for a, b, number in total_runs[blk]}
+        for blk in range(BLOCKS):
+            for d in range(TURNED):
+                for a, b, number in total_runs[blk]:
+                    turn(total[blk, a][:], relu_T[blk, d][:, a:b], d == 0, d == TURNED - 1)
+
         shifted = {blk: keep.tile([P, V], F32, name="shifted%d" % blk) for blk in range(BLOCKS)}
         for blk in range(BLOCKS):
-            nc.vector.tensor_tensor(shifted[blk][:], last[:, blk * V : (blk + 1) * V], s_cen[blk][:], ALU.add)
+            nc.vector.tensor_tensor(shifted[blk][:], scaled[blk, TURNED][:], s_cen[blk][:], ALU.add)
         for blk in range(BLOCKS):
-            for (a, b), src in zip(total_runs[blk], total[blk]):
+            for a, b, number in total_runs[blk]:
                 result = keep.tile([P, b - a], F32, name="result%d_%d" % (blk, a))
-                nc.vector.scalar_tensor_tensor(result[:], shifted[blk][:, a:b], 0.0, src[:], ALU.max, ALU.add)
+                nc.vector.scalar_tensor_tensor(result[:], shifted[blk][:, a:b], 0.0, total[blk, a][:], ALU.max, ALU.add)
                 nc.sync.dma_start(out[P * blk : P * (blk + 1), a:b], result[:])

@@ -25,7 +25,8 @@ TURNED = 2
 HALF = S // 2
 QUARTER = S // 4
 HALVES = [(0, HALF), (HALF, S)]
-QUARTERS = [(a * QUARTER, (a + 1) * QUARTER) for a in (0, 2, 1, 3)]
+QUARTERS = [(a * QUARTER, (a + 1) * QUARTER) for a in (0, 1, 3, 2)]
+DIRECT = 320
 
 
 def tile_picked_filmg_relu_e_kernel(
@@ -50,15 +51,13 @@ def tile_picked_filmg_relu_e_kernel(
         offs_sb = load_list("offs_sb", offs)
         for j in range(1, PACK):
             nc.sync.dma_start(planes[j][:], x_rows[:, j, :])
-        cen_sb = load_list("cen_sb", cen)
-        pos_sb = [load_list("pos%d_sb" % d, src) for d, src in enumerate((pos1, pos2, pos3))]
 
         weights = {"g": (w1_words, w1_scales), "s": (w2_words, w2_scales), "h": (w3_words, w3_scales)}
         words, scales = {}, {}
         for name in "ghs":
             scales[name] = keep.tile([P, N], U8, name="scales_" + name, align_bytes=64)
             words[name] = keep.tile([P, 2 * N], U8, name="words_" + name, align_bytes=64)
-            nc.gpsimd.dma_start(scales[name][0:2, :].bitcast(I32), weights[name][1][0, 0:2, :].bitcast(I32))
+            nc.scalar.dma_start(scales[name][0:2, :].bitcast(I32), weights[name][1][0, 0:2, :].bitcast(I32))
 
         def load_scales(name):
             rows_from_2 = weights[name][1][0, 2:16, :].bitcast(I32)
@@ -70,9 +69,15 @@ def tile_picked_filmg_relu_e_kernel(
         def load_words(name):
             nc.sync.dma_start(words[name][:].bitcast(I32), weights[name][0][0].bitcast(I32))
 
-        for name in "ghs":
-            load_scales(name)
-            load_words(name)
+        load_scales("g")
+        load_words("g")
+        load_scales("h")
+        load_scales("s")
+        cen_sb = load_list("cen_sb", cen)
+        pos_sb = [load_list("pos0_sb", pos1), load_list("pos1_sb", pos2)]
+        load_words("s")
+        load_words("h")
+        pos_sb.append(load_list("pos2_sb", pos3))
 
         zero = keep.tile([P, 1], F32)
         nc.vector.memset(zero[:], 0.0)
@@ -80,21 +85,23 @@ def tile_picked_filmg_relu_e_kernel(
         nc.scalar.activation(ident[:], zero[:].to_broadcast([P, P]), ACT.Copy)
         make_identity(nc, ident[:], nomemset=True)
 
-        woven = [keep.tile([P, PACK * HALF], BF16, name="woven%d" % half, align_bytes=64) for half in range(2)]
-        woven_nodes = [tile[:].rearrange("p (t j) -> p t j", j=PACK) for tile in woven]
-        picked = keep.tile([P, PACK * HALF], BF16, name="picked")
+        woven = keep.tile([P, PACK * S], BF16, name="woven", align_bytes=64)
+        woven_nodes = woven[:].rearrange("p (t j) -> p t j", j=PACK)
+        picked = keep.tile([P, PACK * S], BF16, name="picked")
         picked_nodes = picked[:].rearrange("p (j t) -> p t j", j=PACK)
 
         def plane_at(j, a, b):
             return planes[j][:].indirect(offs_sb[:, a // LIST_ROWS : b // LIST_ROWS])
 
         for j in range(PACK):
-            runs = [(0, QUARTER), (QUARTER, HALF)] if j == PACK - 1 else [(0, HALF)]
+            final = j == PACK - 1
+            for a, b in [(0, QUARTER), (QUARTER, DIRECT)] if final else [(0, DIRECT)]:
+                nc.vector.tensor_copy(woven_nodes[:, a:b, j], plane_at(j, a, b))
+            runs = [(3 * QUARTER, S), (DIRECT, 3 * QUARTER)] if final else [(DIRECT, S)]
             for a, b in runs:
-                nc.vector.tensor_copy(woven_nodes[0][:, a:b, j], plane_at(j, a, b))
-                nc.scalar.activation(picked[:, j * HALF + a : j * HALF + b], plane_at(j, HALF + a, HALF + b), ACT.Copy)
-                if j % 2:
-                    nc.scalar.copy(woven_nodes[1][:, a:b, j - 1 : j + 1], picked_nodes[:, a:b, j - 1 : j + 1])
+                nc.scalar.activation(picked[:, j * S + a : j * S + b], plane_at(j, a, b), ACT.Copy)
+            for a, b in runs if j % 2 else []:
+                nc.scalar.copy(woven_nodes[:, a:b, j - 1 : j + 1], picked_nodes[:, a:b, j - 1 : j + 1])
 
         codes = keep.tile([P, S], U32, name="codes", align_bytes=64)
         x_scales = keep.tile([P, S], U8, name="x_scales", align_bytes=64)
@@ -102,7 +109,7 @@ def tile_picked_filmg_relu_e_kernel(
             nc.vector.quantize_mx(
                 out=codes[:, a:b].bitcast(FP8X4),
                 scales=x_scales[:, a:b],
-                in_=woven[a // HALF][:, PACK * (a % HALF) : PACK * (a % HALF + QUARTER)],
+                in_=woven[:, PACK * a : PACK * b],
             )
 
         rows = {
@@ -137,16 +144,16 @@ def tile_picked_filmg_relu_e_kernel(
             product("g", 0, run, 2 * n, on_s)
             product("g", 1, run, 2 * n + 1, on_v)
         g_cen[0] = centre("g", 0, on_s)
-        g_cen[1] = centre("g", 1, on_v)
-        product("h", 0, HALVES[0], 0, on_s)
-        product("h", 0, HALVES[1], 1, on_v)
-        product("h", 1, HALVES[0], 2, on_s)
-        product("h", 1, HALVES[1], 3, on_s)
+        g_cen[1] = centre("g", 1, on_s)
+        for n, run in enumerate(QUARTERS):
+            product("h", 0, run, n, on_v)
+        product("h", 1, HALVES[0], 4, on_v)
+        product("h", 1, HALVES[1], 5, on_v)
         for blk in range(BLOCKS):
             for half in range(2):
-                product("s", blk, HALVES[half], 4 + 2 * blk + half, on_s)
-        for blk in range(BLOCKS):
-            s_cen[blk] = centre("s", blk, on_s)
+                product("s", blk, HALVES[half], 2 * blk + half, on_s)
+        s_cen[0] = centre("s", 0, on_s)
+        s_cen[1] = centre("s", 1, on_s)
         def turn(dst, src, start, stop):
             squares = src.shape[1] // P
             for a in range(squares):
@@ -160,21 +167,21 @@ def tile_picked_filmg_relu_e_kernel(
                     stop=stop and a == squares - 1,
                 )
 
-        def scaled_neighbour(blk, d):
-            tile = keep.tile([P, V], F32, name="scaled%d_%d" % (blk, d))
-            nc.vector.tensor_tensor(tile[:], rows["h", blk][:].indirect(pos_sb[d][:]), g_cen[blk][:], ALU.mult)
-            return tile
+        def scale_neighbour(dst, blk, d):
+            nc.vector.tensor_tensor(dst, rows["h", blk][:].indirect(pos_sb[d][:]), g_cen[blk][:], ALU.mult)
 
-        shifted_banks = {(0, 0): 4, (0, 1): 5, (1, 0): 6, (1, 1): 7}
+        shifted_banks = {(0, 0): 6, (0, 1): 7, (1, 0): 4, (1, 1): 5}
         total_runs = {0: [(0, V, 0)], 1: [(0, P, 1), (P, V, 2)]}
         scaled, shifted_T, relu_T = {}, {}, {}
         for blk in range(BLOCKS):
             for d in range(TURNED):
-                scaled[blk, d] = scaled_neighbour(blk, d)
+                scaled[blk, d] = keep.tile([P, V], F32, name="scaled%d_%d" % (blk, d))
+                scale_neighbour(scaled[blk, d][:], blk, d)
                 shifted_T[blk, d] = bank(shifted_banks[blk, d], V)
                 turn(shifted_T[blk, d][:], scaled[blk, d][:], True, False)
+        last = keep.tile([P, BLOCKS * V], F32, name="scaled0_1")
         for blk in range(BLOCKS):
-            scaled[blk, TURNED] = scaled_neighbour(blk, TURNED)
+            scale_neighbour(last[:, blk * V : (blk + 1) * V], blk, TURNED)
         for blk in range(BLOCKS):
             for d in range(TURNED):
                 turn(shifted_T[blk, d][:], s_cen[blk][:], False, True)
@@ -188,7 +195,7 @@ def tile_picked_filmg_relu_e_kernel(
 
         shifted = {blk: keep.tile([P, V], F32, name="shifted%d" % blk) for blk in range(BLOCKS)}
         for blk in range(BLOCKS):
-            nc.vector.tensor_tensor(shifted[blk][:], scaled[blk, TURNED][:], s_cen[blk][:], ALU.add)
+            nc.vector.tensor_tensor(shifted[blk][:], last[:, blk * V : (blk + 1) * V], s_cen[blk][:], ALU.add)
         for blk in range(BLOCKS):
             for a, b, number in total_runs[blk]:
                 result = keep.tile([P, b - a], F32, name="result%d_%d" % (blk, a))

@@ -74,10 +74,9 @@ def tile_picked_filmg_relu_e_kernel(
         load_scales("h")
         load_scales("s")
         cen_sb = load_list("cen_sb", cen)
-        pos_sb = [load_list("pos0_sb", pos1), load_list("pos1_sb", pos2)]
         load_words("s")
         load_words("h")
-        pos_sb.append(load_list("pos2_sb", pos3))
+        pos_sb = [load_list("pos%d_sb" % d, src) for d, src in enumerate((pos1, pos2, pos3))]
 
         zero = keep.tile([P, 1], F32)
         nc.vector.memset(zero[:], 0.0)
@@ -113,8 +112,11 @@ def tile_picked_filmg_relu_e_kernel(
             )
 
         rows = {
-            (name, blk): keep.tile([P, S], F32, name="rows_%s%d" % (name, blk)) for blk in range(BLOCKS) for name in "gsh"
+            (name, blk): keep.tile([P, S], F32, name="rows_%s%d" % (name, blk))[:] for blk in range(BLOCKS) for name in "gh"
         }
+        rows_s = keep.tile([P, BLOCKS * S], F32, name="rows_s")
+        for blk in range(BLOCKS):
+            rows["s", blk] = rows_s[:, blk * S : (blk + 1) * S]
 
         def scalar_copy(dst, src):
             nc.scalar.activation(dst, src, ACT.Copy)
@@ -135,69 +137,69 @@ def tile_picked_filmg_relu_e_kernel(
 
         def centre(name, blk, copy):
             tile = keep.tile([P, V], F32, name="%s_cen%d" % (name, blk))
-            copy(tile[:], rows[name, blk][:].indirect(cen_sb[:]))
+            window = rows_s[:] if (name, blk) == ("s", 0) else rows[name, blk]
+            copy(tile[:], window.indirect(cen_sb[:]))
             return tile
 
         on_v, on_s = nc.vector.tensor_copy, scalar_copy
         g_cen, s_cen = {}, {}
-        for n, run in enumerate(QUARTERS):
-            product("g", 0, run, 2 * n, on_s)
-            product("g", 1, run, 2 * n + 1, on_v)
+        for half in range(2):
+            for n in range(2):
+                product("g", 0, QUARTERS[2 * half + n], 3 * half + n, on_s)
+            product("g", 1, HALVES[half], 3 * half + 2, on_v)
         g_cen[0] = centre("g", 0, on_s)
         g_cen[1] = centre("g", 1, on_s)
-        for n, run in enumerate(QUARTERS):
-            product("h", 0, run, n, on_v)
-        product("h", 1, HALVES[0], 4, on_v)
-        product("h", 1, HALVES[1], 5, on_v)
+        for blk in range(BLOCKS):
+            for half in range(2):
+                product("h", blk, HALVES[half], 2 * blk + half, on_v)
         for blk in range(BLOCKS):
             for half in range(2):
                 product("s", blk, HALVES[half], 2 * blk + half, on_s)
         s_cen[0] = centre("s", 0, on_s)
         s_cen[1] = centre("s", 1, on_s)
+        squares = [slice(a * P, (a + 1) * P) for a in range(V // P)]
+
         def turn(dst, src, start, stop):
-            squares = src.shape[1] // P
-            for a in range(squares):
-                square = slice(a * P, (a + 1) * P)
-                nc.tensor.matmul(
-                    dst[:, square],
-                    lhsT=src[:, square],
-                    rhs=ident[:],
-                    is_transpose=True,
-                    start=start and a == 0,
-                    stop=stop and a == squares - 1,
-                )
+            nc.tensor.matmul(dst, lhsT=src, rhs=ident[:], is_transpose=True, start=start, stop=stop)
 
         def scale_neighbour(dst, blk, d):
-            nc.vector.tensor_tensor(dst, rows["h", blk][:].indirect(pos_sb[d][:]), g_cen[blk][:], ALU.mult)
+            nc.vector.tensor_tensor(dst, rows["h", blk].indirect(pos_sb[d][:]), g_cen[blk][:], ALU.mult)
 
         shifted_banks = {(0, 0): 6, (0, 1): 7, (1, 0): 4, (1, 1): 5}
-        total_runs = {0: [(0, V, 0)], 1: [(0, P, 1), (P, V, 2)]}
-        scaled, shifted_T, relu_T = {}, {}, {}
+        total_banks = {(0, 0): 0, (0, 1): 1, (1, 0): 2, (1, 1): 3}
+        shifted_T = {key: bank(number, TURNED * P) for key, number in shifted_banks.items()}
         for blk in range(BLOCKS):
             for d in range(TURNED):
-                scaled[blk, d] = keep.tile([P, V], F32, name="scaled%d_%d" % (blk, d))
-                scale_neighbour(scaled[blk, d][:], blk, d)
-                shifted_T[blk, d] = bank(shifted_banks[blk, d], V)
-                turn(shifted_T[blk, d][:], scaled[blk, d][:], True, False)
+                scaled = keep.tile([P, V], F32, name="scaled%d_%d" % (blk, d))
+                scale_neighbour(scaled[:], blk, d)
+                for a, square in enumerate(squares):
+                    turn(shifted_T[blk, a][:, squares[d]], scaled[:, square], d == 0, False)
         last = keep.tile([P, BLOCKS * V], F32, name="scaled0_1")
         for blk in range(BLOCKS):
             scale_neighbour(last[:, blk * V : (blk + 1) * V], blk, TURNED)
+        relu_T = {}
         for blk in range(BLOCKS):
-            for d in range(TURNED):
-                turn(shifted_T[blk, d][:], s_cen[blk][:], False, True)
-                relu_T[blk, d] = keep.tile([P, V], F32, name="relu_T%d_%d" % (blk, d))
-                nc.scalar.activation(relu_T[blk, d][:], shifted_T[blk, d][:], ACT.Relu)
-        total = {(blk, a): bank(number, b - a) for blk in range(BLOCKS) for a, b, number in total_runs[blk]}
+            for a, square in enumerate(squares):
+                for d in range(TURNED):
+                    turn(shifted_T[blk, a][:, squares[d]], s_cen[blk][:, square], False, d == TURNED - 1)
+                relu_T[blk, a] = keep.tile([P, TURNED * P], F32, name="relu_T%d_%d" % (blk, a))
+                nc.scalar.activation(relu_T[blk, a][:], shifted_T[blk, a][:], ACT.Relu)
+        total = {key: bank(number, P) for key, number in total_banks.items()}
         for blk in range(BLOCKS):
-            for d in range(TURNED):
-                for a, b, number in total_runs[blk]:
-                    turn(total[blk, a][:], relu_T[blk, d][:, a:b], d == 0, d == TURNED - 1)
+            for a in range(len(squares)):
+                for d in range(TURNED):
+                    turn(total[blk, a][:], relu_T[blk, a][:, squares[d]], d == 0, d == TURNED - 1)
 
         shifted = {blk: keep.tile([P, V], F32, name="shifted%d" % blk) for blk in range(BLOCKS)}
         for blk in range(BLOCKS):
             nc.vector.tensor_tensor(shifted[blk][:], last[:, blk * V : (blk + 1) * V], s_cen[blk][:], ALU.add)
+        result = {blk: keep.tile([P, V], F32, name="result%d" % blk) for blk in range(BLOCKS)}
         for blk in range(BLOCKS):
-            for a, b, number in total_runs[blk]:
-                result = keep.tile([P, b - a], F32, name="result%d_%d" % (blk, a))
-                nc.vector.scalar_tensor_tensor(result[:], shifted[blk][:, a:b], 0.0, total[blk, a][:], ALU.max, ALU.add)
-                nc.sync.dma_start(out[P * blk : P * (blk + 1), a:b], result[:])
+            for a, square in enumerate(squares):
+                nc.vector.scalar_tensor_tensor(
+                    result[blk][:, square], shifted[blk][:, square], 0.0, total[blk, a][:], ALU.max, ALU.add
+                )
+                if blk == BLOCKS - 1:
+                    nc.sync.dma_start(out[P * blk : P * (blk + 1), square], result[blk][:, square])
+            if blk < BLOCKS - 1:
+                nc.sync.dma_start(out[P * blk : P * (blk + 1), :], result[blk][:])

@@ -74,9 +74,10 @@ def tile_picked_filmg_relu_e_kernel(
         load_scales("h")
         load_scales("s")
         cen_sb = load_list("cen_sb", cen)
+        pos_sb = [load_list("pos0_sb", pos1), load_list("pos1_sb", pos2)]
         load_words("s")
         load_words("h")
-        pos_sb = [load_list("pos%d_sb" % d, src) for d, src in enumerate((pos1, pos2, pos3))]
+        pos_sb.append(load_list("pos2_sb", pos3))
 
         zero = keep.tile([P, 1], F32)
         nc.vector.memset(zero[:], 0.0)
@@ -138,7 +139,8 @@ def tile_picked_filmg_relu_e_kernel(
         def centre(name, blk, copy):
             tile = keep.tile([P, V], F32, name="%s_cen%d" % (name, blk))
             window = rows_s[:] if (name, blk) == ("s", 0) else rows[name, blk]
-            copy(tile[:], window.indirect(cen_sb[:]))
+            for a, b in [(0, P), (P, V)] if name == "s" else [(0, V)]:
+                copy(tile[:, a:b], window.indirect(cen_sb[:, a // LIST_ROWS : b // LIST_ROWS]))
             return tile
 
         on_v, on_s = nc.vector.tensor_copy, scalar_copy
@@ -168,12 +170,14 @@ def tile_picked_filmg_relu_e_kernel(
         shifted_banks = {(0, 0): 6, (0, 1): 7, (1, 0): 4, (1, 1): 5}
         total_banks = {(0, 0): 0, (0, 1): 1, (1, 0): 2, (1, 1): 3}
         shifted_T = {key: bank(number, TURNED * P) for key, number in shifted_banks.items()}
+        scaled, latest = {}, (BLOCKS - 1, TURNED - 1)
         for blk in range(BLOCKS):
             for d in range(TURNED):
-                scaled = keep.tile([P, V], F32, name="scaled%d_%d" % (blk, d))
-                scale_neighbour(scaled[:], blk, d)
+                scaled[blk, d] = keep.tile([P, V], F32, name="scaled%d_%d" % (blk, d))
+                scale_neighbour(scaled[blk, d][:], blk, d)
                 for a, square in enumerate(squares):
-                    turn(shifted_T[blk, a][:, squares[d]], scaled[:, square], d == 0, False)
+                    if (blk, d) != latest:
+                        turn(shifted_T[blk, a][:, squares[d]], scaled[blk, d][:, square], d == 0, False)
         last = keep.tile([P, BLOCKS * V], F32, name="scaled0_1")
         for blk in range(BLOCKS):
             scale_neighbour(last[:, blk * V : (blk + 1) * V], blk, TURNED)
@@ -181,7 +185,9 @@ def tile_picked_filmg_relu_e_kernel(
         for blk in range(BLOCKS):
             for a, square in enumerate(squares):
                 for d in range(TURNED):
-                    turn(shifted_T[blk, a][:, squares[d]], s_cen[blk][:, square], False, d == TURNED - 1)
+                    turn(shifted_T[blk, a][:, squares[d]], s_cen[blk][:, square], False, blk == 0 and d == TURNED - 1)
+                if blk == BLOCKS - 1:
+                    turn(shifted_T[blk, a][:, squares[d]], scaled[latest][:, square], False, True)
                 relu_T[blk, a] = keep.tile([P, TURNED * P], F32, name="relu_T%d_%d" % (blk, a))
                 nc.scalar.activation(relu_T[blk, a][:], shifted_T[blk, a][:], ACT.Relu)
         total = {key: bank(number, P) for key, number in total_banks.items()}

@@ -26,7 +26,7 @@ HALF = S // 2
 QUARTER = S // 4
 HALVES = [(0, HALF), (HALF, S)]
 QUARTERS = [(a * QUARTER, (a + 1) * QUARTER) for a in (0, 1, 3, 2)]
-DIRECT = 320
+DIRECT = (256, 288)
 
 
 def tile_picked_filmg_relu_e_kernel(
@@ -94,10 +94,10 @@ def tile_picked_filmg_relu_e_kernel(
             return planes[j][:].indirect(offs_sb[:, a // LIST_ROWS : b // LIST_ROWS])
 
         for j in range(PACK):
-            final = j == PACK - 1
-            for a, b in [(0, QUARTER), (QUARTER, DIRECT)] if final else [(0, DIRECT)]:
+            final, direct = j == PACK - 1, DIRECT[j // 2]
+            for a, b in [(0, QUARTER), (QUARTER, direct)] if final else [(0, direct)]:
                 nc.vector.tensor_copy(woven_nodes[:, a:b, j], plane_at(j, a, b))
-            runs = [(3 * QUARTER, S), (DIRECT, 3 * QUARTER)] if final else [(DIRECT, S)]
+            runs = [(3 * QUARTER, S), (direct, 3 * QUARTER)] if final else [(direct, S)]
             for a, b in runs:
                 nc.scalar.activation(picked[:, j * S + a : j * S + b], plane_at(j, a, b), ACT.Copy)
             for a, b in runs if j % 2 else []:

@@ -26,7 +26,7 @@ HALF = S // 2
 QUARTER = S // 4
 HALVES = [(0, HALF), (HALF, S)]
 QUARTERS = [(a * QUARTER, (a + 1) * QUARTER) for a in (0, 1, 3, 2)]
-DIRECT = (256, 288)
+DIRECT = 288
 
 
 def tile_picked_filmg_relu_e_kernel(
@@ -94,10 +94,10 @@ def tile_picked_filmg_relu_e_kernel(
             return planes[j][:].indirect(offs_sb[:, a // LIST_ROWS : b // LIST_ROWS])
 
         for j in range(PACK):
-            final, direct = j == PACK - 1, DIRECT[j // 2]
+            final, direct = j == PACK - 1, DIRECT
             for a, b in [(0, QUARTER), (QUARTER, direct)] if final else [(0, direct)]:
                 nc.vector.tensor_copy(woven_nodes[:, a:b, j], plane_at(j, a, b))
-            runs = [(3 * QUARTER, S), (direct, 3 * QUARTER)] if final else [(direct, S)]
+            runs = [(3 * QUARTER, S), (direct, 3 * QUARTER)] if j % 2 else [(direct, S)]
             for a, b in runs:
                 nc.scalar.activation(picked[:, j * S + a : j * S + b], plane_at(j, a, b), ACT.Copy)
             for a, b in runs if j % 2 else []:
@@ -113,11 +113,8 @@ def tile_picked_filmg_relu_e_kernel(
             )
 
         rows = {
-            (name, blk): keep.tile([P, S], F32, name="rows_%s%d" % (name, blk))[:] for blk in range(BLOCKS) for name in "gh"
+            (name, blk): keep.tile([P, S], F32, name="rows_%s%d" % (name, blk))[:] for blk in range(BLOCKS) for name in "ghs"
         }
-        rows_s = keep.tile([P, BLOCKS * S], F32, name="rows_s")
-        for blk in range(BLOCKS):
-            rows["s", blk] = rows_s[:, blk * S : (blk + 1) * S]
 
         def scalar_copy(dst, src):
             nc.scalar.activation(dst, src, ACT.Copy)
@@ -138,9 +135,8 @@ def tile_picked_filmg_relu_e_kernel(
 
         def centre(name, blk, copy):
             tile = keep.tile([P, V], F32, name="%s_cen%d" % (name, blk))
-            window = rows_s[:] if (name, blk) == ("s", 0) else rows[name, blk]
             for a, b in [(0, P), (P, V)] if name == "s" else [(0, V)]:
-                copy(tile[:, a:b], window.indirect(cen_sb[:, a // LIST_ROWS : b // LIST_ROWS]))
+                copy(tile[:, a:b], rows[name, blk].indirect(cen_sb[:, a // LIST_ROWS : b // LIST_ROWS]))
             return tile
 
         on_v, on_s = nc.vector.tensor_copy, scalar_copy

@@ -163,9 +163,13 @@ def tile_picked_filmg_relu_e_kernel(
         def scale_neighbour(dst, blk, d):
             nc.vector.tensor_tensor(dst, rows["h", blk].indirect(pos_sb[d][:]), g_cen[blk][:], ALU.mult)
 
-        shifted_banks = {(0, 0): 6, (0, 1): 7, (1, 0): 4, (1, 1): 5}
-        total_banks = {(0, 0): 0, (0, 1): 1, (1, 0): 2, (1, 1): 3}
-        shifted_T = {key: bank(number, TURNED * P) for key, number in shifted_banks.items()}
+        groups = {(0, 0, (0, 1)): 6, (0, 1, (0, 1)): 7, (1, 0, (0, 1)): 4, (1, 1, (0,)): 5, (1, 1, (1,)): 3}
+        shifted_T, closes = {}, {}
+        for (blk, a, ds), number in groups.items():
+            tile = bank(number, len(ds) * P)
+            for n, d in enumerate(ds):
+                shifted_T[blk, a, d] = tile[:, squares[n]]
+            closes[blk, a, ds] = tile
         scaled, latest = {}, (BLOCKS - 1, TURNED - 1)
         for blk in range(BLOCKS):
             for d in range(TURNED):
@@ -173,35 +177,37 @@ def tile_picked_filmg_relu_e_kernel(
                 scale_neighbour(scaled[blk, d][:], blk, d)
                 for a, square in enumerate(squares):
                     if (blk, d) != latest:
-                        turn(shifted_T[blk, a][:, squares[d]], scaled[blk, d][:, square], d == 0, False)
+                        turn(shifted_T[blk, a, d], scaled[blk, d][:, square], d == 0, False)
         last = keep.tile([P, BLOCKS * V], F32, name="scaled0_1")
         for blk in range(BLOCKS):
             scale_neighbour(last[:, blk * V : (blk + 1) * V], blk, TURNED)
         relu_T = {}
-        for blk in range(BLOCKS):
-            for a, square in enumerate(squares):
-                for d in range(TURNED):
-                    turn(shifted_T[blk, a][:, squares[d]], s_cen[blk][:, square], False, blk == 0 and d == TURNED - 1)
-                if blk == BLOCKS - 1:
-                    turn(shifted_T[blk, a][:, squares[d]], scaled[latest][:, square], False, True)
-                relu_T[blk, a] = keep.tile([P, TURNED * P], F32, name="relu_T%d_%d" % (blk, a))
-                nc.scalar.activation(relu_T[blk, a][:], shifted_T[blk, a][:], ACT.Relu)
-        total = {key: bank(number, P) for key, number in total_banks.items()}
+        for (blk, a, ds), tile in closes.items():
+            with_latest = (blk, ds[-1]) == latest
+            for d in ds:
+                turn(shifted_T[blk, a, d], s_cen[blk][:, squares[a]], ds == (1,), d == ds[-1] and not with_latest)
+            if with_latest:
+                turn(shifted_T[blk, a, ds[-1]], scaled[latest][:, squares[a]], False, True)
+            relu = keep.tile([P, len(ds) * P], F32, name="relu_T%d_%d_%d" % (blk, a, ds[0]))
+            nc.scalar.activation(relu[:], tile[:], ACT.Relu)
+            for n, d in enumerate(ds):
+                relu_T[blk, a, d] = relu[:, squares[n]]
+        total0 = bank(0, V)
+        total = {(0, a): total0[:, square] for a, square in enumerate(squares)}
+        total.update({(1, a): bank(1 + a, P)[:] for a in range(len(squares))})
         for blk in range(BLOCKS):
             for a in range(len(squares)):
                 for d in range(TURNED):
-                    turn(total[blk, a][:], relu_T[blk, a][:, squares[d]], d == 0, d == TURNED - 1)
+                    turn(total[blk, a], relu_T[blk, a, d], d == 0, d == TURNED - 1)
 
         shifted = {blk: keep.tile([P, V], F32, name="shifted%d" % blk) for blk in range(BLOCKS)}
         for blk in range(BLOCKS):
             nc.vector.tensor_tensor(shifted[blk][:], last[:, blk * V : (blk + 1) * V], s_cen[blk][:], ALU.add)
         result = {blk: keep.tile([P, V], F32, name="result%d" % blk) for blk in range(BLOCKS)}
-        for blk in range(BLOCKS):
-            for a, square in enumerate(squares):
-                nc.vector.scalar_tensor_tensor(
-                    result[blk][:, square], shifted[blk][:, square], 0.0, total[blk, a][:], ALU.max, ALU.add
-                )
-                if blk == BLOCKS - 1:
-                    nc.sync.dma_start(out[P * blk : P * (blk + 1), square], result[blk][:, square])
-            if blk < BLOCKS - 1:
-                nc.sync.dma_start(out[P * blk : P * (blk + 1), :], result[blk][:])
+        nc.vector.scalar_tensor_tensor(result[0][:], shifted[0][:], 0.0, total0[:], ALU.max, ALU.add)
+        nc.sync.dma_start(out[0:P, :], result[0][:])
+        for a, square in enumerate(squares):
+            nc.vector.scalar_tensor_tensor(
+                result[1][:, square], shifted[1][:, square], 0.0, total[1, a], ALU.max, ALU.add
+            )
+            nc.sync.dma_start(out[P : 2 * P, square], result[1][:, square])

@@ -25,8 +25,8 @@ TURNED = 2
 HALF = S // 2
 QUARTER = S // 4
 HALVES = [(0, HALF), (HALF, S)]
-QUARTERS = [(a * QUARTER, (a + 1) * QUARTER) for a in (0, 1, 3, 2)]
-DIRECT = 288
+QUARTERS = [(a * QUARTER, (a + 1) * QUARTER) for a in (3, 0, 1, 2)]
+DIRECT = 192
 
 
 def tile_picked_filmg_relu_e_kernel(
@@ -87,21 +87,16 @@ def tile_picked_filmg_relu_e_kernel(
 
         woven = keep.tile([P, PACK * S], BF16, name="woven", align_bytes=64)
         woven_nodes = woven[:].rearrange("p (t j) -> p t j", j=PACK)
-        picked = keep.tile([P, PACK * S], BF16, name="picked")
-        picked_nodes = picked[:].rearrange("p (j t) -> p t j", j=PACK)
 
         def plane_at(j, a, b):
             return planes[j][:].indirect(offs_sb[:, a // LIST_ROWS : b // LIST_ROWS])
 
         for j in range(PACK):
-            final, direct = j == PACK - 1, DIRECT
-            for a, b in [(0, QUARTER), (QUARTER, direct)] if final else [(0, direct)]:
-                nc.vector.tensor_copy(woven_nodes[:, a:b, j], plane_at(j, a, b))
-            runs = [(3 * QUARTER, S), (direct, 3 * QUARTER)] if j % 2 else [(direct, S)]
+            direct = DIRECT if j >= 2 else HALF
+            nc.vector.tensor_copy(woven_nodes[:, 0:direct, j], plane_at(j, 0, direct))
+            runs = [QUARTERS[0], (direct, HALF), QUARTERS[3]] if j == PACK - 1 else [(direct, S)]
             for a, b in runs:
-                nc.scalar.activation(picked[:, j * S + a : j * S + b], plane_at(j, a, b), ACT.Copy)
-            for a, b in runs if j % 2 else []:
-                nc.scalar.copy(woven_nodes[:, a:b, j - 1 : j + 1], picked_nodes[:, a:b, j - 1 : j + 1])
+                nc.scalar.activation(woven_nodes[:, a:b, j], plane_at(j, a, b), ACT.Copy)
 
         codes = keep.tile([P, S], U32, name="codes", align_bytes=64)
         x_scales = keep.tile([P, S], U8, name="x_scales", align_bytes=64)
@@ -141,10 +136,11 @@ def tile_picked_filmg_relu_e_kernel(
 
         on_v, on_s = nc.vector.tensor_copy, scalar_copy
         g_cen, s_cen = {}, {}
-        for half in range(2):
-            for n in range(2):
-                product("g", 0, QUARTERS[2 * half + n], 3 * half + n, on_s)
-            product("g", 1, HALVES[half], 3 * half + 2, on_v)
+        for run, number in zip(QUARTERS[:3], (0, 1, 3)):
+            product("g", 0, run, number, on_s)
+        product("g", 1, HALVES[0], 2, on_v)
+        product("g", 0, QUARTERS[3], 4, on_s)
+        product("g", 1, HALVES[1], 5, on_v)
         g_cen[0] = centre("g", 0, on_s)
         g_cen[1] = centre("g", 1, on_s)
         for blk in range(BLOCKS):

@@ -74,10 +74,9 @@ def tile_picked_filmg_relu_e_kernel(
         load_scales("h")
         load_scales("s")
         cen_sb = load_list("cen_sb", cen)
-        pos_sb = [load_list("pos0_sb", pos1), load_list("pos1_sb", pos2)]
         load_words("s")
         load_words("h")
-        pos_sb.append(load_list("pos2_sb", pos3))
+        pos_sb = [load_list("pos%d_sb" % d, pos) for d, pos in enumerate((pos1, pos2, pos3))]
 
         zero = keep.tile([P, 1], F32)
         nc.vector.memset(zero[:], 0.0)
@@ -136,16 +135,18 @@ def tile_picked_filmg_relu_e_kernel(
 
         on_v, on_s = nc.vector.tensor_copy, scalar_copy
         g_cen, s_cen = {}, {}
-        for run, number in zip(QUARTERS[:3], (0, 1, 3)):
+        product("g", 0, QUARTERS[0], 0, on_s)
+        product("g", 1, QUARTERS[0], 6, on_v)
+        for run, number in zip(QUARTERS[1:3], (1, 3)):
             product("g", 0, run, number, on_s)
-        product("g", 1, HALVES[0], 2, on_v)
+        product("g", 1, QUARTERS[1], 2, on_v)
         product("g", 0, QUARTERS[3], 4, on_s)
-        product("g", 1, HALVES[1], 5, on_v)
+        product("g", 1, (QUARTER, 3 * QUARTER), 5, on_v)
         g_cen[0] = centre("g", 0, on_s)
         g_cen[1] = centre("g", 1, on_s)
-        for blk in range(BLOCKS):
-            for half in range(2):
-                product("h", blk, HALVES[half], 2 * blk + half, on_v)
+        for number, (blk, run) in enumerate([(0, HALVES[0]), (0, HALVES[1]), (1, HALVES[0]), (1, QUARTERS[3])]):
+            product("h", blk, run, number, on_v)
+        product("h", 1, QUARTERS[0], 7, on_s)
         for blk in range(BLOCKS):
             for half in range(2):
                 product("s", blk, HALVES[half], 2 * blk + half, on_s)

@@ -129,7 +129,7 @@ def tile_picked_filmg_relu_e_kernel(
 
         def centre(name, blk, copy):
             tile = keep.tile([P, V], F32, name="%s_cen%d" % (name, blk))
-            for a, b in [(0, P), (P, V)] if name == "s" else [(0, V)]:
+            for a, b in [(0, P), (P, V)] if (name, blk) == ("s", 1) else [(0, V)]:
                 copy(tile[:, a:b], rows[name, blk].indirect(cen_sb[:, a // LIST_ROWS : b // LIST_ROWS]))
             return tile
 
@@ -137,19 +137,18 @@ def tile_picked_filmg_relu_e_kernel(
         g_cen, s_cen = {}, {}
         product("g", 0, QUARTERS[0], 0, on_s)
         product("g", 1, QUARTERS[0], 6, on_v)
-        for run, number in zip(QUARTERS[1:3], (1, 3)):
-            product("g", 0, run, number, on_s)
+        for run, number in zip(QUARTERS[1:], (1, 3, 4)):
+            product("g", 0, run, number, on_v if run == QUARTERS[-1] else on_s)
         product("g", 1, QUARTERS[1], 2, on_v)
-        product("g", 0, QUARTERS[3], 4, on_s)
         product("g", 1, (QUARTER, 3 * QUARTER), 5, on_v)
         g_cen[0] = centre("g", 0, on_s)
         g_cen[1] = centre("g", 1, on_s)
         for number, (blk, run) in enumerate([(0, HALVES[0]), (0, HALVES[1]), (1, HALVES[0]), (1, QUARTERS[3])]):
             product("h", blk, run, number, on_v)
         product("h", 1, QUARTERS[0], 7, on_s)
-        for blk in range(BLOCKS):
-            for half in range(2):
-                product("s", blk, HALVES[half], 2 * blk + half, on_s)
+        for half in range(2):
+            product("s", 0, HALVES[half], half, on_s)
+        product("s", 1, (0, S), 2, on_s)
         s_cen[0] = centre("s", 0, on_s)
         s_cen[1] = centre("s", 1, on_s)
         squares = [slice(a * P, (a + 1) * P) for a in range(V // P)]

@@ -143,9 +143,9 @@ def tile_picked_filmg_relu_e_kernel(
         product("g", 1, (QUARTER, 3 * QUARTER), 5, on_v)
         g_cen[0] = centre("g", 0, on_s)
         g_cen[1] = centre("g", 1, on_s)
-        for number, (blk, run) in enumerate([(0, HALVES[0]), (0, HALVES[1]), (1, HALVES[0]), (1, QUARTERS[3])]):
+        for number, (blk, run) in enumerate([(0, HALVES[0]), (0, HALVES[1]), (1, HALVES[0])]):
             product("h", blk, run, number, on_v)
-        product("h", 1, QUARTERS[0], 7, on_s)
+        product("h", 1, HALVES[1], 3, on_s)
         for half in range(2):
             product("s", 0, HALVES[half], half, on_s)
         product("s", 1, (0, S), 2, on_s)

@@ -26,7 +26,7 @@ HALF = S // 2
 QUARTER = S // 4
 HALVES = [(0, HALF), (HALF, S)]
 QUARTERS = [(a * QUARTER, (a + 1) * QUARTER) for a in (3, 0, 1, 2)]
-DIRECT = 192
+DIRECT = 160
 
 
 def tile_picked_filmg_relu_e_kernel(
@@ -69,13 +69,12 @@ def tile_picked_filmg_relu_e_kernel(
         def load_words(name):
             nc.sync.dma_start(words[name][:].bitcast(I32), weights[name][0][0].bitcast(I32))
 
-        load_scales("g")
-        load_words("g")
-        load_scales("h")
-        load_scales("s")
+        for name in "gh":
+            load_scales(name)
+            load_words(name)
         cen_sb = load_list("cen_sb", cen)
+        load_scales("s")
         load_words("s")
-        load_words("h")
         pos_sb = [load_list("pos%d_sb" % d, pos) for d, pos in enumerate((pos1, pos2, pos3))]
 
         zero = keep.tile([P, 1], F32)
@@ -143,9 +142,9 @@ def tile_picked_filmg_relu_e_kernel(
         product("g", 1, (QUARTER, 3 * QUARTER), 5, on_v)
         g_cen[0] = centre("g", 0, on_s)
         g_cen[1] = centre("g", 1, on_s)
-        for number, (blk, run) in enumerate([(0, HALVES[0]), (0, HALVES[1]), (1, HALVES[0])]):
+        for number, (blk, run) in enumerate([(0, HALVES[0]), (0, HALVES[1]), (1, HALVES[0]), (1, QUARTERS[3])]):
             product("h", blk, run, number, on_v)
-        product("h", 1, HALVES[1], 3, on_s)
+        product("h", 1, QUARTERS[0], 7, on_s)
         for half in range(2):
             product("s", 0, HALVES[half], half, on_s)
         product("s", 1, (0, S), 2, on_s)
@@ -174,7 +173,7 @@ def tile_picked_filmg_relu_e_kernel(
                 for a, square in enumerate(squares):
                     if (blk, d) != latest:
                         turn(shifted_T[blk, a, d], scaled[blk, d][:, square], d == 0, False)
-        last = keep.tile([P, BLOCKS * V], F32, name="scaled0_1")
+        last = keep.tile([P, BLOCKS * V], F32, name="last")
         for blk in range(BLOCKS):
             scale_neighbour(last[:, blk * V : (blk + 1) * V], blk, TURNED)
         relu_T = {}

@@ -142,12 +142,11 @@ def tile_picked_filmg_relu_e_kernel(
         product("g", 1, (QUARTER, 3 * QUARTER), 5, on_v)
         g_cen[0] = centre("g", 0, on_s)
         g_cen[1] = centre("g", 1, on_s)
-        for number, (blk, run) in enumerate([(0, HALVES[0]), (0, HALVES[1]), (1, HALVES[0]), (1, QUARTERS[3])]):
+        for number, (blk, run) in enumerate([(0, HALVES[0]), (0, HALVES[1]), (1, HALVES[0]), (1, HALVES[1])]):
             product("h", blk, run, number, on_v)
-        product("h", 1, QUARTERS[0], 7, on_s)
-        for half in range(2):
-            product("s", 0, HALVES[half], half, on_s)
-        product("s", 1, (0, S), 2, on_s)
+        for blk in range(BLOCKS):
+            for half in range(2):
+                product("s", blk, HALVES[half], 2 * blk + half, on_s)
         s_cen[0] = centre("s", 0, on_s)
         s_cen[1] = centre("s", 1, on_s)
         squares = [slice(a * P, (a + 1) * P) for a in range(V // P)]

from contextlib import ExitStack

import concourse.mybir as mybir
from concourse.masks import make_identity

K, T, S, V, N = 512, 1024, 512, 256, 256
FLOPS = 3 * 2 * K * S * N

F32 = mybir.dt.float32
BF16 = mybir.dt.bfloat16
I32 = mybir.dt.int32
U32 = mybir.dt.uint32
U16 = mybir.dt.uint16
U8 = mybir.dt.uint8
FP8X4 = mybir.dt.float8_e4m3fn_x4
FP4X4 = mybir.dt.float4_e2m1fn_x4
ALU = mybir.AluOpType
ACT = mybir.ActivationFunctionType

P = 128
PACK = 4
LIST_ROWS = 16
BLOCKS = N // P
TURNED = 2
HALF = S // 2
QUARTER = S // 4
HALVES = [(0, HALF), (HALF, S)]
QUARTERS = [(a * QUARTER, (a + 1) * QUARTER) for a in (3, 0, 1, 2)]
DIRECT = 160


def tile_picked_filmg_relu_e_kernel(
    tc, xT, w1_words, w1_scales, w2_words, w2_scales, w3_words, w3_scales, offs, cen, pos1, pos2, pos3, out
):
    nc = tc.nc
    with ExitStack() as ctx:
        keep = ctx.enter_context(tc.tile_pool(name="keep", bufs=1))
        psum = ctx.enter_context(tc.psum_pool(name="psum", bufs=1))

        def bank(number, width):
            return psum.tile([P, width], F32, name="bank%d" % number)

        def load_list(name, src):
            tile = keep.tile(list(src.shape), U16, name=name)
            nc.sync.dma_start(tile[:], src)
            return tile

        x_rows = xT.rearrange("(p j) t -> p j t", j=PACK)
        planes = [keep.tile([P, T], F32, name="plane%d" % j) for j in range(PACK)]
        nc.sync.dma_start(planes[0][:], x_rows[:, 0, :])
        offs_sb = load_list("offs_sb", offs)
        for j in range(1, PACK):
            nc.sync.dma_start(planes[j][:], x_rows[:, j, :])

        weights = {"g": (w1_words, w1_scales), "s": (w2_words, w2_scales), "h": (w3_words, w3_scales)}
        words, scales = {}, {}
        for name in "ghs":
            scales[name] = keep.tile([P, N], U8, name="scales_" + name, align_bytes=64)
            words[name] = keep.tile([P, 2 * N], U8, name="words_" + name, align_bytes=64)
            nc.scalar.dma_start(scales[name][0:2, :].bitcast(I32), weights[name][1][0, 0:2, :].bitcast(I32))

        def load_scales(name):
            rows_from_2 = weights[name][1][0, 2:16, :].bitcast(I32)
            nc.sync.dma_start(
                scales[name][2:P, :].bitcast(I32),
                rows_from_2.unsqueeze(0).to_broadcast([(P - 2) // 14, 14, N // 4]),
            )

        def load_words(name):
            nc.sync.dma_start(words[name][:].bitcast(I32), weights[name][0][0].bitcast(I32))

        for name in "gh":
            load_scales(name)
            load_words(name)
        cen_sb = load_list("cen_sb", cen)
        load_scales("s")
        load_words("s")
        pos_sb = [load_list("pos%d_sb" % d, pos) for d, pos in enumerate((pos1, pos2, pos3))]

        zero = keep.tile([P, 1], F32)
        nc.vector.memset(zero[:], 0.0)
        ident = keep.tile([P, P], F32)
        nc.scalar.activation(ident[:], zero[:].to_broadcast([P, P]), ACT.Copy)
        make_identity(nc, ident[:], nomemset=True)

        woven = keep.tile([P, PACK * S], BF16, name="woven", align_bytes=64)
        woven_nodes = woven[:].rearrange("p (t j) -> p t j", j=PACK)

        def plane_at(j, a, b):
            return planes[j][:].indirect(offs_sb[:, a // LIST_ROWS : b // LIST_ROWS])

        for j in range(PACK):
            direct = DIRECT if j >= 2 else HALF
            nc.vector.tensor_copy(woven_nodes[:, 0:direct, j], plane_at(j, 0, direct))
            runs = [QUARTERS[0], (direct, HALF), QUARTERS[3]] if j == PACK - 1 else [(direct, S)]
            for a, b in runs:
                nc.scalar.activation(woven_nodes[:, a:b, j], plane_at(j, a, b), ACT.Copy)

        codes = keep.tile([P, S], U32, name="codes", align_bytes=64)
        x_scales = keep.tile([P, S], U8, name="x_scales", align_bytes=64)
        for a, b in QUARTERS:
            nc.vector.quantize_mx(
                out=codes[:, a:b].bitcast(FP8X4),
                scales=x_scales[:, a:b],
                in_=woven[:, PACK * a : PACK * b],
            )

        rows = {
            (name, blk): keep.tile([P, S], F32, name="rows_%s%d" % (name, blk))[:] for blk in range(BLOCKS) for name in "ghs"
        }

        def scalar_copy(dst, src):
            nc.scalar.activation(dst, src, ACT.Copy)

        def product(name, blk, run, number, copy_out):
            a, b = run
            piece = bank(number, b - a)
            nc.tensor.matmul_mx(
                out=piece[:],
                lhsT=words[name][:, 2 * P * blk : 2 * P * (blk + 1)].bitcast(FP4X4),
                lhsT_scale=scales[name][:, P * blk : P * (blk + 1)],
                rhs=codes[:, a:b].bitcast(FP8X4),
                rhs_scale=x_scales[:, a:b],
                start=True,
                stop=True,
            )
            copy_out(rows[name, blk][:, a:b], piece[:])

        def centre(name, blk, copy):
            tile = keep.tile([P, V], F32, name="%s_cen%d" % (name, blk))
            for a, b in [(0, P), (P, V)] if (name, blk) == ("s", 1) else [(0, V)]:
                copy(tile[:, a:b], rows[name, blk].indirect(cen_sb[:, a // LIST_ROWS : b // LIST_ROWS]))
            return tile

        on_v, on_s = nc.vector.tensor_copy, scalar_copy
        g_cen, s_cen = {}, {}
        product("g", 0, QUARTERS[0], 0, on_s)
        product("g", 1, QUARTERS[0], 6, on_v)
        for run, number in zip(QUARTERS[1:], (1, 3, 4)):
            product("g", 0, run, number, on_v if run == QUARTERS[-1] else on_s)
        product("g", 1, QUARTERS[1], 2, on_v)
        product("g", 1, (QUARTER, 3 * QUARTER), 5, on_v)
        g_cen[0] = centre("g", 0, on_s)
        g_cen[1] = centre("g", 1, on_s)
        for number, (blk, run) in enumerate([(0, HALVES[0]), (0, HALVES[1]), (1, HALVES[0]), (1, HALVES[1])]):
            product("h", blk, run, number, on_v)
        for blk in range(BLOCKS):
            for half in range(2):
                product("s", blk, HALVES[half], 2 * blk + half, on_s)
        s_cen[0] = centre("s", 0, on_s)
        s_cen[1] = centre("s", 1, on_s)
        squares = [slice(a * P, (a + 1) * P) for a in range(V // P)]

        def turn(dst, src, start, stop):
            nc.tensor.matmul(dst, lhsT=src, rhs=ident[:], is_transpose=True, start=start, stop=stop)

        def scale_neighbour(dst, blk, d):
            nc.vector.tensor_tensor(dst, rows["h", blk].indirect(pos_sb[d][:]), g_cen[blk][:], ALU.mult)

        groups = {(0, 0, (0, 1)): 6, (0, 1, (0, 1)): 7, (1, 0, (0, 1)): 4, (1, 1, (0,)): 5, (1, 1, (1,)): 3}
        shifted_T, closes = {}, {}
        for (blk, a, ds), number in groups.items():
            tile = bank(number, len(ds) * P)
            for n, d in enumerate(ds):
                shifted_T[blk, a, d] = tile[:, squares[n]]
            closes[blk, a, ds] = tile
        scaled, latest = {}, (BLOCKS - 1, TURNED - 1)
        for blk in range(BLOCKS):
            for d in range(TURNED):
                scaled[blk, d] = keep.tile([P, V], F32, name="scaled%d_%d" % (blk, d))
                scale_neighbour(scaled[blk, d][:], blk, d)
                for a, square in enumerate(squares):
                    if (blk, d) != latest:
                        turn(shifted_T[blk, a, d], scaled[blk, d][:, square], d == 0, False)
        last = keep.tile([P, BLOCKS * V], F32, name="last")
        for blk in range(BLOCKS):
            scale_neighbour(last[:, blk * V : (blk + 1) * V], blk, TURNED)
        relu_T = {}
        for (blk, a, ds), tile in closes.items():
            with_latest = (blk, ds[-1]) == latest
            for d in ds:
                turn(shifted_T[blk, a, d], s_cen[blk][:, squares[a]], ds == (1,), d == ds[-1] and not with_latest)
            if with_latest:
                turn(shifted_T[blk, a, ds[-1]], scaled[latest][:, squares[a]], False, True)
            relu = keep.tile([P, len(ds) * P], F32, name="relu_T%d_%d_%d" % (blk, a, ds[0]))
            nc.scalar.activation(relu[:], tile[:], ACT.Relu)
            for n, d in enumerate(ds):
                relu_T[blk, a, d] = relu[:, squares[n]]
        total0 = bank(0, V)
        total = {(0, a): total0[:, square] for a, square in enumerate(squares)}
        total.update({(1, a): bank(1 + a, P)[:] for a in range(len(squares))})
        for blk in range(BLOCKS):
            for a in range(len(squares)):
                for d in range(TURNED):
                    turn(total[blk, a], relu_T[blk, a, d], d == 0, d == TURNED - 1)

        shifted = {blk: keep.tile([P, V], F32, name="shifted%d" % blk) for blk in range(BLOCKS)}
        for blk in range(BLOCKS):
            nc.vector.tensor_tensor(shifted[blk][:], last[:, blk * V : (blk + 1) * V], s_cen[blk][:], ALU.add)
        result = {blk: keep.tile([P, V], F32, name="result%d" % blk) for blk in range(BLOCKS)}
        nc.vector.scalar_tensor_tensor(result[0][:], shifted[0][:], 0.0, total0[:], ALU.max, ALU.add)
        nc.sync.dma_start(out[0:P, :], result[0][:])
        for a, square in enumerate(squares):
            nc.vector.scalar_tensor_tensor(
                result[1][:, square], shifted[1][:, square], 0.0, total[1, a], ALU.max, ALU.add
            )
            nc.sync.dma_start(out[P : 2 * P, square], result[1][:, square])
